import numpy as np
import ml_dtypes


def mxq(x, axis, fmt="e4m3"):
    dtype, down = {"e4m3": (ml_dtypes.float8_e4m3fn, 7), "e5m2": (ml_dtypes.float8_e5m2, 14)}[fmt]
    v = np.moveaxis(np.asarray(x, np.float32).astype(ml_dtypes.bfloat16).astype(np.float64), axis, -1)
    blocks = v.reshape(v.shape[:-1] + (-1, 32))
    amax = np.abs(blocks).max(-1, keepdims=True)
    byte = np.maximum(np.where(amax > 0, np.frexp(amax)[1] - 1 + 127, 0) - down, 1)
    scale = np.exp2(byte - 127.0)
    codes = (blocks / scale).astype(np.float32).astype(dtype).astype(np.float64)
    return np.moveaxis((codes * scale).reshape(v.shape), -1, axis)


WIDE = False


def mx_kscale(k):
    if not WIDE:
        return np.ones(k)
    levels = np.array([10, -10, 5, -5, 0])
    if k % 512:
        return np.exp2(np.random.permutation(np.resize(levels, k // 32))).repeat(32)
    a = np.empty((k // 512, 16))
    for p in range(k // 512):
        a[p, :8] = np.random.permutation(np.resize(levels, 8))
        for g in range(8):
            far = levels[np.abs(levels - a[p, g]) >= 10]
            a[p, g + 8] = far[np.random.randint(len(far))]
    return np.exp2(a.ravel()).repeat(32)


def f64(x):
    return np.asarray(x).astype(np.float64)


def striped(idx):
    return np.tile(idx.reshape(-1, 16).T, (8, 1)).astype(np.uint16)


def unstriped(offs):
    return offs[:16].T.reshape(-1).astype(np.int64)


E2M1 = np.array([0.0, 0.5, 1.0, 1.5, 2.0, 3.0, 4.0, 6.0, -0.0, -0.5, -1.0, -1.5, -2.0, -3.0, -4.0, -6.0])


def pack_weight(w, fmt):
    k, n = w.shape
    w = f64(np.asarray(w, np.float32).astype(ml_dtypes.bfloat16)).reshape(k // 32, 32, n)
    amax = np.abs(w).max(1)
    if fmt == "e4m3":
        byte = np.frexp(amax)[1] - 1 + 127 - 7
    else:
        mant, ex = np.frexp(amax / 6.0)
        byte = np.where(mant > 0.5, ex, ex - 1) + 127
    byte = np.clip(np.where(amax > 0, byte, 1), 1, 254)
    scaled = (w * np.exp2(127.0 - byte)[:, None, :]).reshape(k, n).astype(np.float32)
    by_word = np.ascontiguousarray(scaled.reshape(k // 512, 128, 4, n).transpose(0, 1, 3, 2))
    if fmt == "e4m3":
        words = by_word.astype(ml_dtypes.float8_e4m3fn).view(np.uint8)
    else:
        c = by_word.astype(ml_dtypes.float4_e2m1fn).view(np.uint8) & 0xF
        words = (c[..., 0::2] | (c[..., 1::2] << 4)).reshape(k // 512, 128, 2 * n)
    return np.ascontiguousarray(words), np.ascontiguousarray(byte.astype(np.uint8).reshape(k // 512, 16, n))


def unpack_weight(words, scales, fmt):
    g, _, n = scales.shape
    words = np.ascontiguousarray(words).reshape(g, 128, n, -1)
    if fmt == "e4m3":
        vals = words.view(ml_dtypes.float8_e4m3fn).astype(np.float64)
    else:
        nib = np.empty((g, 128, n, 4), np.uint8)
        nib[..., 0::2] = words & 0xF
        nib[..., 1::2] = words >> 4
        vals = E2M1[nib]
    vals = vals * np.repeat(np.exp2(scales.astype(np.float64) - 127.0), 8, axis=1)[..., None]
    return vals.transpose(0, 1, 3, 2).reshape(g * 512, n)


K, T, E, C, N = 2560, 640, 6, 128, 256
R = 4


def by_expert(wq, xq):
    return np.concatenate([wq[e].T @ xq[:, e * C:(e + 1) * C] for e in range(E)], axis=1)


def setup_inputs():
    n = np.random.standard_normal
    s = mx_kscale(K)[:, None]
    slot_token = np.concatenate([r * (T // R) + np.random.permutation(T // R)[:C // R] for e in range(E) for r in range(R)])
    w = [pack_weight(m, "e2m1") for m in n((E, K, N)) / np.sqrt(K) / s[None]]
    return {
        "xT": (n((K, T)) * s).astype(np.float32),
        "w_words": np.stack([m[0] for m in w]),
        "w_scales": np.stack([m[1] for m in w]),
        "offs": striped(slot_token),
    }


def reference(xT, w_words, w_scales, offs):
    idx = unstriped(offs)
    w = np.stack([unpack_weight(w_words[e], w_scales[e], "e2m1") for e in range(E)])
    xq = mxq(f64(xT)[:, idx], 0, "e4m3")
    y = by_expert(w, xq)
    return y.reshape(N, E, R, C // R).transpose(0, 2, 1, 3).reshape(N, E * C)

@@ -1,0 +1,166 @@
+from contextlib import ExitStack
+
+import concourse.mybir as mybir
+
+K, T, E, C, N = 2560, 640, 6, 128, 256
+R = 4
+S = E * C
+P = 128
+A = K // 512
+U = C // R
+
+F32 = mybir.dt.float32
+BF16 = mybir.dt.bfloat16
+I32 = mybir.dt.int32
+U32 = mybir.dt.uint32
+U16 = mybir.dt.uint16
+U8 = mybir.dt.uint8
+FP8X4 = mybir.dt.float8_e4m3fn_x4
+FP4X4 = mybir.dt.float4_e2m1fn_x4
+
+FLOPS = 2 * K * N * S
+
+WINDOW = 1024
+FIRST_ROW = [4, 8, 12, 0]
+SCALAR_COLS = [224, 384, 512, 544, 576]
+SHIFT_ROWS = 112
+
+
+def tile_moe_eps_lin_none_kernel(tc, xT, w_words, w_scales, offs, out):
+    nc = tc.nc
+    with ExitStack() as ctx:
+        keep = ctx.enter_context(tc.tile_pool(name="keep", bufs=1))
+        psum = ctx.enter_context(tc.psum_pool(name="psum", bufs=8))
+
+        offsets = keep.tile([P, S // 16], U16, name="offsets")
+        raw = [keep.tile([P, 4, T], F32, name=f"raw{a}") for a in range(A)]
+        grouped = [keep.tile([P, T * 4], BF16, name=f"grouped{a}", align_bytes=64) for a in range(A)]
+        codes = [keep.tile([P, T], I32, name=f"codes{a}", align_bytes=64) for a in range(A)]
+        packed = keep.tile([P, WINDOW], U8, name="packed", align_bytes=64)
+        single = keep.tile([P, T], U8, name="single", align_bytes=64)
+        slot_words = [keep.tile([P, S], I32, name=f"slot_words{a}", align_bytes=64) for a in range(A)]
+        slot_packed = keep.tile([P, S], U8, name="slot_packed", align_bytes=64)
+        slot_single = keep.tile([P, S], U8, name="slot_single", align_bytes=64)
+        shifted = [keep.tile([P, S], U8, name=f"shifted{a}", align_bytes=64) for a in range(3)]
+        weights = [keep.tile([P, A * 2 * N], U8, name=f"weights{e}", align_bytes=64) for e in range(E)]
+        w_planes = keep.tile([P, E * A * N], U8, name="w_planes", align_bytes=64)
+        result = [keep.tile([P, S], F32, name=f"result{h}") for h in range(2)]
+
+        for a in range(A):
+            nc.sync.dma_start(out=raw[a][:], in_=xT[512 * a : 512 * (a + 1), :].rearrange("(p j) t -> p j t", j=4))
+            if a == 0:
+                nc.sync.dma_start(offsets[:], offs)
+        nc.gpsimd.memset(w_planes[:].bitcast(I32), 0)
+        for r in range(4):
+            nc.sync.dma_start(
+                out=w_planes[r:P:32, :].bitcast(I32).rearrange("q (g n) -> q g n", g=E * A),
+                in_=w_scales[:, :, r:16:4, :].bitcast(I32).rearrange("e a q n -> q (e a) n"),
+            )
+        nc.vector.memset(packed[:].bitcast(I32), 0)
+        nc.vector.memset(single[:].bitcast(I32), 0)
+        for a in range(3):
+            nc.gpsimd.memset(shifted[a][:].bitcast(I32), 0)
+        for e in range(E):
+            nc.sync.dma_start(
+                out=weights[e][:].bitcast(I32).rearrange("p (a n) -> p a n", a=A),
+                in_=w_words[e].bitcast(I32).rearrange("a p n -> p a n"),
+            )
+
+        def interleave(a, engine_copy, lo, hi):
+            engine_copy(
+                out=grouped[a][:, 4 * lo : 4 * hi].rearrange("p (c i j) -> p c j i", i=4, j=4),
+                in_=raw[a][:, :, lo:hi].rearrange("p j (c i) -> p c j i", i=4),
+            )
+
+        def quantise(a, lo, hi):
+            if a < 4:
+                plane = packed[FIRST_ROW[a] : P, lo:hi]
+            else:
+                plane = single[:, lo:hi]
+            nc.vector.quantize_mx(out=codes[a][:, lo:hi].bitcast(FP8X4), scales=plane, in_=grouped[a][:, 4 * lo : 4 * hi])
+
+        def gather_words(a, lo, hi):
+            nc.vector.tensor_copy(
+                slot_words[a][:, lo:hi].bitcast(U32),
+                codes[a][:].bitcast(U32).indirect(offsets[:, lo // 16 : hi // 16]),
+            )
+
+        def gather_bytes(dst, src, lo, hi):
+            nc.vector.tensor_copy(dst[:, lo:hi], src[:].indirect(offsets[:, lo // 16 : hi // 16]))
+
+        for a in range(A):
+            cut = SCALAR_COLS[a]
+            mid = 320 if a == 4 else cut
+            interleave(a, nc.scalar.copy, 0, mid)
+            if a == 4:
+                for b in range(3):
+                    first = FIRST_ROW[b]
+                    nc.scalar.dma_start(
+                        out=shifted[b][0:SHIFT_ROWS, :].bitcast(I32),
+                        in_=slot_packed[first : first + SHIFT_ROWS, :].bitcast(I32),
+                    )
+                interleave(a, nc.scalar.copy, mid, cut)
+            interleave(a, nc.vector.tensor_copy, cut, T)
+            quantise(a, 0, 512)
+            quantise(a, 512, T)
+            if a > 0:
+                gather_words(a - 1, 480, S)
+            if a == 3:
+                gather_bytes(slot_packed, packed, 0, S)
+            if a < 4:
+                gather_words(a, 0, 480)
+        for lo in (0, 256, 512):
+            gather_bytes(slot_single, single, lo, lo + 256)
+            gather_words(4, lo, lo + 256)
+
+        planes = shifted + [slot_packed, slot_single]
+        accs = {}
+
+        def multiply(e, h, a, start, stop):
+            words = weights[e][:, 512 * a + 256 * h : 512 * a + 256 * h + 256]
+            g = (e * A + a) * N + 128 * h
+            slots = slice(C * e, C * (e + 1))
+            nc.tensor.matmul_mx(
+                out=accs[e, h][:],
+                lhsT=words.bitcast(FP4X4),
+                lhsT_scale=w_planes[:, g : g + 128],
+                rhs=slot_words[a][:, slots].bitcast(FP8X4),
+                rhs_scale=planes[a][:, slots],
+                start=start,
+                stop=stop,
+            )
+
+        def leave(e, h, engine_copy):
+            engine_copy(
+                out=result[h][:].rearrange("p (m e u) -> p m e u", m=R, e=E)[:, :, e, :],
+                in_=accs[e, h][:].rearrange("p (m u) -> p m u", m=R),
+            )
+
+        for e in range(4):
+            for h in range(2):
+                accs[e, h] = psum.tile([P, C], F32, name="acc")
+                multiply(e, h, 3, True, False)
+        for e in range(4):
+            for a in range(3):
+                for h in range(2):
+                    multiply(e, h, a, False, False)
+        for e in (0, 1):
+            for h in range(2):
+                multiply(e, h, 4, False, True)
+                leave(e, h, nc.scalar.copy)
+        for e in (4, 5):
+            for h in range(2):
+                accs[e, h] = psum.tile([P, C], F32, name="acc")
+                for a in (3, 0, 1, 2):
+                    multiply(e, h, a, a == 3, False)
+        for e in (2, 3):
+            for h in range(2):
+                multiply(e, h, 4, False, True)
+                leave(e, h, nc.scalar.copy)
+        for e in (4, 5):
+            for h in range(2):
+                multiply(e, h, 4, False, True)
+            leave(e, 0, nc.scalar.copy)
+            leave(e, 1, nc.vector.tensor_copy)
+        nc.sync.dma_start(out=out[0:P, :], in_=result[0][:])
+        nc.scalar.dma_start(out=out[P : 2 * P, :], in_=result[1][:])

@@ -8,6 +8,7 @@ S = E * C
 P = 128
 A = K // 512
 U = C // R
+W = 2 * N
 
 F32 = mybir.dt.float32
 BF16 = mybir.dt.bfloat16
@@ -20,9 +21,8 @@ FP4X4 = mybir.dt.float4_e2m1fn_x4
 
 FLOPS = 2 * K * N * S
 
-WINDOW = 1024
-FIRST_ROW = [4, 8, 12, 0]
-SCALAR_COLS = [224, 384, 512, 544, 576]
+FIRST_ROW = {1: 0, 2: 4, 3: 8}
+SCALAR_COLS = [224, 640, 640, 640, 640]
 SHIFT_ROWS = 112
 
 
@@ -30,41 +30,45 @@ def tile_moe_eps_lin_none_kernel(tc, xT, w_words, w_scales, offs, out):
     nc = tc.nc
     with ExitStack() as ctx:
         keep = ctx.enter_context(tc.tile_pool(name="keep", bufs=1))
-        psum = ctx.enter_context(tc.psum_pool(name="psum", bufs=8))
+        psum = ctx.enter_context(tc.psum_pool(name="psum", bufs=1))
 
         offsets = keep.tile([P, S // 16], U16, name="offsets")
-        raw = [keep.tile([P, 4, T], F32, name=f"raw{a}") for a in range(A)]
         grouped = [keep.tile([P, T * 4], BF16, name=f"grouped{a}", align_bytes=64) for a in range(A)]
         codes = [keep.tile([P, T], I32, name=f"codes{a}", align_bytes=64) for a in range(A)]
-        packed = keep.tile([P, WINDOW], U8, name="packed", align_bytes=64)
-        single = keep.tile([P, T], U8, name="single", align_bytes=64)
+        packed = keep.tile([P, T], U8, name="packed", align_bytes=64)
+        single = {a: keep.tile([P, T], U8, name=f"single{a}", align_bytes=64) for a in (0, 4)}
         slot_words = [keep.tile([P, S], I32, name=f"slot_words{a}", align_bytes=64) for a in range(A)]
         slot_packed = keep.tile([P, S], U8, name="slot_packed", align_bytes=64)
-        slot_single = keep.tile([P, S], U8, name="slot_single", align_bytes=64)
-        shifted = [keep.tile([P, S], U8, name=f"shifted{a}", align_bytes=64) for a in range(3)]
-        weights = [keep.tile([P, A * 2 * N], U8, name=f"weights{e}", align_bytes=64) for e in range(E)]
+        slot_single = {a: keep.tile([P, S], U8, name=f"slot_single{a}", align_bytes=64) for a in (0, 4)}
+        shifted = {a: keep.tile([P, S], U8, name=f"shifted{a}", align_bytes=64) for a in (2, 3)}
         w_planes = keep.tile([P, E * A * N], U8, name="w_planes", align_bytes=64)
-        result = [keep.tile([P, S], F32, name=f"result{h}") for h in range(2)]
+        early = [keep.tile([P, R, 4 * U], F32, name=f"early{h}") for h in range(2)]
+        last = [keep.tile([P, R, 2 * U], F32, name=f"last{h}") for h in range(2)]
+        accs = {(g, h): psum.tile([P, 2 * C], F32, name=f"acc{g}{h}") for g in range(3) for h in range(2)}
+        raw = {}
+        weights = {}
 
-        for a in range(A):
+        def load_x(a):
+            raw[a] = keep.tile([P, 4, T], F32, name=f"raw{a}", tag=f"raw{a}", align_bytes=64)
             nc.sync.dma_start(out=raw[a][:], in_=xT[512 * a : 512 * (a + 1), :].rearrange("(p j) t -> p j t", j=4))
-            if a == 0:
-                nc.sync.dma_start(offsets[:], offs)
-        nc.gpsimd.memset(w_planes[:].bitcast(I32), 0)
-        for r in range(4):
+
+        def load_first_passes(held):
+            for a in (0, 1):
+                part = held[:, a * E * W : (a + 1) * E * W]
+                nc.sync.dma_start(
+                    out=part.bitcast(I32).rearrange("p (e n) -> p e n", e=E),
+                    in_=w_words[:, a].bitcast(I32).rearrange("e p n -> p e n"),
+                )
+                for e in range(E):
+                    weights[e, a] = part[:, e * W : (e + 1) * W]
+
+        def load_last_passes(e, part):
             nc.sync.dma_start(
-                out=w_planes[r:P:32, :].bitcast(I32).rearrange("q (g n) -> q g n", g=E * A),
-                in_=w_scales[:, :, r:16:4, :].bitcast(I32).rearrange("e a q n -> q (e a) n"),
+                out=part.bitcast(I32).rearrange("p (a n) -> p a n", a=3),
+                in_=w_words[e, 2:A].bitcast(I32).rearrange("a p n -> p a n"),
             )
-        nc.vector.memset(packed[:].bitcast(I32), 0)
-        nc.vector.memset(single[:].bitcast(I32), 0)
-        for a in range(3):
-            nc.gpsimd.memset(shifted[a][:].bitcast(I32), 0)
-        for e in range(E):
-            nc.sync.dma_start(
-                out=weights[e][:].bitcast(I32).rearrange("p (a n) -> p a n", a=A),
-                in_=w_words[e].bitcast(I32).rearrange("a p n -> p a n"),
-            )
+            for a in range(2, A):
+                weights[e, a] = part[:, (a - 2) * W : (a - 1) * W]
 
         def interleave(a, engine_copy, lo, hi):
             engine_copy(
@@ -72,12 +76,14 @@ def tile_moe_eps_lin_none_kernel(tc, xT, w_words, w_scales, offs, out):
                 in_=raw[a][:, :, lo:hi].rearrange("p j (c i) -> p c j i", i=4),
             )
 
-        def quantise(a, lo, hi):
-            if a < 4:
-                plane = packed[FIRST_ROW[a] : P, lo:hi]
-            else:
-                plane = single[:, lo:hi]
-            nc.vector.quantize_mx(out=codes[a][:, lo:hi].bitcast(FP8X4), scales=plane, in_=grouped[a][:, 4 * lo : 4 * hi])
+        def quantise(a):
+            cut = SCALAR_COLS[a]
+            interleave(a, nc.scalar.copy, 0, cut)
+            if cut < T:
+                interleave(a, nc.vector.tensor_copy, cut, T)
+            for lo, hi in ((0, 512), (512, T)):
+                plane = packed[FIRST_ROW[a] : P, lo:hi] if a in FIRST_ROW else single[a][:, lo:hi]
+                nc.vector.quantize_mx(out=codes[a][:, lo:hi].bitcast(FP8X4), scales=plane, in_=grouped[a][:, 4 * lo : 4 * hi])
 
         def gather_words(a, lo, hi):
             nc.vector.tensor_copy(
@@ -88,79 +94,86 @@ def tile_moe_eps_lin_none_kernel(tc, xT, w_words, w_scales, offs, out):
         def gather_bytes(dst, src, lo, hi):
             nc.vector.tensor_copy(dst[:, lo:hi], src[:].indirect(offsets[:, lo // 16 : hi // 16]))
 
+        nc.vector.memset(w_planes[:].bitcast(I32), 0)
+        for plane in [packed, single[0], single[4], shifted[2], shifted[3]]:
+            nc.vector.memset(plane[:].bitcast(I32), 0)
+        load_x(0)
+        nc.sync.dma_start(offsets[:], offs)
+        for a in range(1, A):
+            load_x(a)
+        for r in range(4):
+            nc.sync.dma_start(
+                out=w_planes[r:P:32, :].bitcast(I32).rearrange("q (g n) -> q g n", g=E * A),
+                in_=w_scales[:, :, r:16:4, :].bitcast(I32).rearrange("e a q n -> q (e a) n"),
+            )
+        halves = ((0, S // 2), (S // 2, S))
         for a in range(A):
-            cut = SCALAR_COLS[a]
-            mid = 320 if a == 4 else cut
-            interleave(a, nc.scalar.copy, 0, mid)
-            if a == 4:
-                for b in range(3):
-                    first = FIRST_ROW[b]
-                    nc.scalar.dma_start(
-                        out=shifted[b][0:SHIFT_ROWS, :].bitcast(I32),
-                        in_=slot_packed[first : first + SHIFT_ROWS, :].bitcast(I32),
-                    )
-                interleave(a, nc.scalar.copy, mid, cut)
-            interleave(a, nc.vector.tensor_copy, cut, T)
-            quantise(a, 0, 512)
-            quantise(a, 512, T)
-            if a > 0:
-                gather_words(a - 1, 480, S)
+            quantise(a)
+            if a == 0:
+                held = keep.tile([P, (2 * E + 2 * 3) * W], U8, name="first_weights", tag="raw0", align_bytes=64)
+                load_first_passes(held)
+                for e in (0, 1):
+                    load_last_passes(e, held[:, (2 * E + 3 * e) * W : (2 * E + 3 * e + 3) * W])
             if a == 3:
-                gather_bytes(slot_packed, packed, 0, S)
+                for lo, hi in halves:
+                    gather_bytes(slot_packed, packed, lo, hi)
             if a < 4:
-                gather_words(a, 0, 480)
+                for lo, hi in halves:
+                    gather_words(a, lo, hi)
+            if a == 0:
+                for lo, hi in halves:
+                    gather_bytes(slot_single[a], single[a], lo, hi)
+        for b in (2, 3):
+            first = FIRST_ROW[b]
+            nc.scalar.dma_start(
+                out=shifted[b][0:SHIFT_ROWS, :].bitcast(I32),
+                in_=slot_packed[first : first + SHIFT_ROWS, :].bitcast(I32),
+            )
+        held = keep.tile([P, 4 * 3 * W], U8, name="last_weights", tag="raw4", align_bytes=64)
+        for e in range(2, E):
+            load_last_passes(e, held[:, 3 * (e - 2) * W : 3 * (e - 1) * W])
         for lo in (0, 256, 512):
-            gather_bytes(slot_single, single, lo, lo + 256)
+            gather_bytes(slot_single[4], single[4], lo, lo + 256)
             gather_words(4, lo, lo + 256)
 
-        planes = shifted + [slot_packed, slot_single]
-        accs = {}
+        planes = [slot_single[0], slot_packed, shifted[2], shifted[3], slot_single[4]]
 
-        def multiply(e, h, a, start, stop):
-            words = weights[e][:, 512 * a + 256 * h : 512 * a + 256 * h + 256]
-            g = (e * A + a) * N + 128 * h
+        def multiply(e, h, a):
+            words = weights[e, a][:, 256 * h : 256 * h + 256]
+            col = (e * A + a) * N + 128 * h
             slots = slice(C * e, C * (e + 1))
             nc.tensor.matmul_mx(
-                out=accs[e, h][:],
+                out=accs[e // 2, h][:, C * (e % 2) : C * (e % 2 + 1)],
                 lhsT=words.bitcast(FP4X4),
-                lhsT_scale=w_planes[:, g : g + 128],
+                lhsT_scale=w_planes[:, col : col + 128],
                 rhs=slot_words[a][:, slots].bitcast(FP8X4),
                 rhs_scale=planes[a][:, slots],
-                start=start,
-                stop=stop,
+                start=(a == 0 and e % 2 == 0),
+                stop=(a == A - 1 and e % 2 == 1),
             )
 
-        def leave(e, h, engine_copy):
+        def leave(g, h, engine_copy):
+            dst = early[h][:, :, 2 * U * g : 2 * U * (g + 1)] if g < 2 else last[h][:]
             engine_copy(
-                out=result[h][:].rearrange("p (m e u) -> p m e u", m=R, e=E)[:, :, e, :],
-                in_=accs[e, h][:].rearrange("p (m u) -> p m u", m=R),
+                out=dst.rearrange("p m (e u) -> p m e u", e=2),
+                in_=accs[g, h][:].rearrange("p (e m u) -> p m e u", e=2, m=R),
             )
 
-        for e in range(4):
-            for h in range(2):
-                accs[e, h] = psum.tile([P, C], F32, name="acc")
-                multiply(e, h, 3, True, False)
-        for e in range(4):
-            for a in range(3):
+        by_rank = out.rearrange("n (m c) -> n m c", m=R)
+        for a in (0, 1):
+            for e in range(E):
                 for h in range(2):
-                    multiply(e, h, a, False, False)
-        for e in (0, 1):
+                    multiply(e, h, a)
+        for g in range(3):
+            for e in (2 * g, 2 * g + 1):
+                for a in (2, 3):
+                    for h in range(2):
+                        multiply(e, h, a)
             for h in range(2):
-                multiply(e, h, 4, False, True)
-                leave(e, h, nc.scalar.copy)
-        for e in (4, 5):
-            for h in range(2):
-                accs[e, h] = psum.tile([P, C], F32, name="acc")
-                for a in (3, 0, 1, 2):
-                    multiply(e, h, a, a == 3, False)
-        for e in (2, 3):
-            for h in range(2):
-                multiply(e, h, 4, False, True)
-                leave(e, h, nc.scalar.copy)
-        for e in (4, 5):
-            for h in range(2):
-                multiply(e, h, 4, False, True)
-            leave(e, 0, nc.scalar.copy)
-            leave(e, 1, nc.vector.tensor_copy)
-        nc.sync.dma_start(out=out[0:P, :], in_=result[0][:])
-        nc.scalar.dma_start(out=out[P : 2 * P, :], in_=result[1][:])
+                for e in (2 * g, 2 * g + 1):
+                    multiply(e, h, 4)
+                leave(g, h, nc.vector.tensor_copy if (g, h) == (2, 1) else nc.scalar.copy)
+                if g == 1:
+                    nc.sync.dma_start(out=by_rank[P * h : P * (h + 1), :, 0 : 4 * U], in_=early[h][:])
+        nc.scalar.dma_start(out=by_rank[0:P, :, 4 * U : 6 * U], in_=last[0][:])
+        nc.sync.dma_start(out=by_rank[P : 2 * P, :, 4 * U : 6 * U], in_=last[1][:])

@@ -21,9 +21,10 @@ FP4X4 = mybir.dt.float4_e2m1fn_x4
 
 FLOPS = 2 * K * N * S
 
-FIRST_ROW = {1: 0, 2: 4, 3: 8}
-SCALAR_COLS = [224, 640, 640, 640, 640]
+FIRST_ROW = {0: 0, 1: 4, 2: 8}
+SCALAR_COLS = [224, 384, 448, 640, 640]
 SHIFT_ROWS = 112
+WINDOW = 1024
 
 
 def tile_moe_eps_lin_none_kernel(tc, xT, w_words, w_scales, offs, out):
@@ -34,13 +35,14 @@ def tile_moe_eps_lin_none_kernel(tc, xT, w_words, w_scales, offs, out):
 
         offsets = keep.tile([P, S // 16], U16, name="offsets")
         grouped = [keep.tile([P, T * 4], BF16, name=f"grouped{a}", align_bytes=64) for a in range(A)]
-        codes = [keep.tile([P, T], I32, name=f"codes{a}", align_bytes=64) for a in range(A)]
-        packed = keep.tile([P, T], U8, name="packed", align_bytes=64)
-        single = {a: keep.tile([P, T], U8, name=f"single{a}", align_bytes=64) for a in (0, 4)}
+        all_codes = keep.tile([P, (A - 1) * T + WINDOW], I32, name="all_codes", align_bytes=64)
+        codes = [all_codes[:, (A - 1 - a) * T : (A - a) * T] for a in range(A)]
+        packed = keep.tile([P, WINDOW], U8, name="packed", tag="late", align_bytes=64)
+        single = {a: keep.tile([P, WINDOW], U8, name=f"single{a}", align_bytes=64) for a in (3, 4)}
         slot_words = [keep.tile([P, S], I32, name=f"slot_words{a}", align_bytes=64) for a in range(A)]
         slot_packed = keep.tile([P, S], U8, name="slot_packed", align_bytes=64)
-        slot_single = {a: keep.tile([P, S], U8, name=f"slot_single{a}", align_bytes=64) for a in (0, 4)}
-        shifted = {a: keep.tile([P, S], U8, name=f"shifted{a}", align_bytes=64) for a in (2, 3)}
+        slot_single = {a: keep.tile([P, S], U8, name=f"slot_single{a}", align_bytes=64) for a in (3, 4)}
+        shifted = {a: keep.tile([P, S], U8, name=f"shifted{a}", align_bytes=64) for a in (1, 2)}
         w_planes = keep.tile([P, E * A * N], U8, name="w_planes", align_bytes=64)
         early = [keep.tile([P, R, 4 * U], F32, name=f"early{h}") for h in range(2)]
         last = [keep.tile([P, R, 2 * U], F32, name=f"last{h}") for h in range(2)]
@@ -52,15 +54,13 @@ def tile_moe_eps_lin_none_kernel(tc, xT, w_words, w_scales, offs, out):
             raw[a] = keep.tile([P, 4, T], F32, name=f"raw{a}", tag=f"raw{a}", align_bytes=64)
             nc.sync.dma_start(out=raw[a][:], in_=xT[512 * a : 512 * (a + 1), :].rearrange("(p j) t -> p j t", j=4))
 
-        def load_first_passes(held):
-            for a in (0, 1):
-                part = held[:, a * E * W : (a + 1) * E * W]
-                nc.sync.dma_start(
-                    out=part.bitcast(I32).rearrange("p (e n) -> p e n", e=E),
-                    in_=w_words[:, a].bitcast(I32).rearrange("e p n -> p e n"),
-                )
-                for e in range(E):
-                    weights[e, a] = part[:, e * W : (e + 1) * W]
+        def load_pass(a, part):
+            nc.sync.dma_start(
+                out=part.bitcast(I32).rearrange("p (e n) -> p e n", e=E),
+                in_=w_words[:, a].bitcast(I32).rearrange("e p n -> p e n"),
+            )
+            for e in range(E):
+                weights[e, a] = part[:, e * W : (e + 1) * W]
 
         def load_last_passes(e, part):
             nc.sync.dma_start(
@@ -88,15 +88,16 @@ def tile_moe_eps_lin_none_kernel(tc, xT, w_words, w_scales, offs, out):
         def gather_words(a, lo, hi):
             nc.vector.tensor_copy(
                 slot_words[a][:, lo:hi].bitcast(U32),
-                codes[a][:].bitcast(U32).indirect(offsets[:, lo // 16 : hi // 16]),
+                all_codes[:, (A - 1 - a) * T : (A - 1 - a) * T + WINDOW].bitcast(U32).indirect(offsets[:, lo // 16 : hi // 16]),
             )
 
         def gather_bytes(dst, src, lo, hi):
             nc.vector.tensor_copy(dst[:, lo:hi], src[:].indirect(offsets[:, lo // 16 : hi // 16]))
 
         nc.vector.memset(w_planes[:].bitcast(I32), 0)
-        for plane in [packed, single[0], single[4], shifted[2], shifted[3]]:
+        for plane in [packed, single[3], single[4], shifted[1], shifted[2]]:
             nc.vector.memset(plane[:].bitcast(I32), 0)
+        nc.vector.memset(all_codes[:, A * T :], 0)
         load_x(0)
         nc.sync.dma_start(offsets[:], offs)
         for a in range(1, A):
@@ -106,37 +107,32 @@ def tile_moe_eps_lin_none_kernel(tc, xT, w_words, w_scales, offs, out):
                 out=w_planes[r:P:32, :].bitcast(I32).rearrange("q (g n) -> q g n", g=E * A),
                 in_=w_scales[:, :, r:16:4, :].bitcast(I32).rearrange("e a q n -> q (e a) n"),
             )
-        halves = ((0, S // 2), (S // 2, S))
         for a in range(A):
             quantise(a)
             if a == 0:
-                held = keep.tile([P, (2 * E + 2 * 3) * W], U8, name="first_weights", tag="raw0", align_bytes=64)
-                load_first_passes(held)
-                for e in (0, 1):
-                    load_last_passes(e, held[:, (2 * E + 3 * e) * W : (2 * E + 3 * e + 3) * W])
-            if a == 3:
-                for lo, hi in halves:
-                    gather_bytes(slot_packed, packed, lo, hi)
+                first_weights = keep.tile([P, E * W], U8, name="first_weights", tag="raw0", align_bytes=64)
+                load_pass(0, first_weights[:])
+            if a == 2:
+                gather_bytes(slot_packed, packed, 0, S)
+                for b in (1, 2):
+                    first = FIRST_ROW[b]
+                    nc.sync.dma_start(
+                        out=shifted[b][0:SHIFT_ROWS, :].bitcast(I32),
+                        in_=slot_packed[first : first + SHIFT_ROWS, :].bitcast(I32),
+                    )
+                held = keep.tile([P, E * (A - 1) * W], U8, name="weights", tag="late", align_bytes=64)
+                load_pass(1, held[:, 0 : E * W])
+                for e in range(E):
+                    load_last_passes(e, held[:, (E + 3 * e) * W : (E + 3 * e + 3) * W])
             if a < 4:
-                for lo, hi in halves:
-                    gather_words(a, lo, hi)
-            if a == 0:
-                for lo, hi in halves:
-                    gather_bytes(slot_single[a], single[a], lo, hi)
-        for b in (2, 3):
-            first = FIRST_ROW[b]
-            nc.scalar.dma_start(
-                out=shifted[b][0:SHIFT_ROWS, :].bitcast(I32),
-                in_=slot_packed[first : first + SHIFT_ROWS, :].bitcast(I32),
-            )
-        held = keep.tile([P, 4 * 3 * W], U8, name="last_weights", tag="raw4", align_bytes=64)
-        for e in range(2, E):
-            load_last_passes(e, held[:, 3 * (e - 2) * W : 3 * (e - 1) * W])
+                gather_words(a, 0, S)
+            if a == 3:
+                gather_bytes(slot_single[a], single[a], 0, S)
         for lo in (0, 256, 512):
             gather_bytes(slot_single[4], single[4], lo, lo + 256)
             gather_words(4, lo, lo + 256)
 
-        planes = [slot_single[0], slot_packed, shifted[2], shifted[3], slot_single[4]]
+        planes = [slot_packed, shifted[1], shifted[2], slot_single[3], slot_single[4]]
 
         def multiply(e, h, a):
             words = weights[e, a][:, 256 * h : 256 * h + 256]

@@ -9,6 +9,9 @@ P = 128
 A = K // 512
 U = C // R
 W = 2 * N
+PAIRS = E // 2
+HALVES = N // P
+LAST = A - 1
 
 F32 = mybir.dt.float32
 BF16 = mybir.dt.bfloat16
@@ -21,10 +24,10 @@ FP4X4 = mybir.dt.float4_e2m1fn_x4
 
 FLOPS = 2 * K * N * S
 
-FIRST_ROW = {0: 0, 1: 4, 2: 8}
-SCALAR_COLS = [224, 384, 448, 640, 640]
-SHIFT_ROWS = 112
+SCALAR_TOKENS = [224, 384, 448, 256, 640]
 WINDOW = 1024
+SHIFT_ROWS = 112
+QUANTISE_CUTS = ((0, 512), (512, T))
 
 
 def tile_moe_eps_lin_none_kernel(tc, xT, w_words, w_scales, offs, out):
@@ -34,19 +37,19 @@ def tile_moe_eps_lin_none_kernel(tc, xT, w_words, w_scales, offs, out):
         psum = ctx.enter_context(tc.psum_pool(name="psum", bufs=1))
 
         offsets = keep.tile([P, S // 16], U16, name="offsets")
-        grouped = [keep.tile([P, T * 4], BF16, name=f"grouped{a}", align_bytes=64) for a in range(A)]
-        all_codes = keep.tile([P, (A - 1) * T + WINDOW], I32, name="all_codes", align_bytes=64)
-        codes = [all_codes[:, (A - 1 - a) * T : (A - a) * T] for a in range(A)]
-        packed = keep.tile([P, WINDOW], U8, name="packed", tag="late", align_bytes=64)
-        single = {a: keep.tile([P, WINDOW], U8, name=f"single{a}", align_bytes=64) for a in (3, 4)}
-        slot_words = [keep.tile([P, S], I32, name=f"slot_words{a}", align_bytes=64) for a in range(A)]
-        slot_packed = keep.tile([P, S], U8, name="slot_packed", align_bytes=64)
-        slot_single = {a: keep.tile([P, S], U8, name=f"slot_single{a}", align_bytes=64) for a in (3, 4)}
-        shifted = {a: keep.tile([P, S], U8, name=f"shifted{a}", align_bytes=64) for a in (1, 2)}
+        grouped = [keep.tile([P, T * 4], BF16, name=f"grouped{a}", tag=f"grouped{a}", align_bytes=64) for a in range(A)]
+        token_words = keep.tile([P, LAST * T + WINDOW], I32, name="token_words", align_bytes=64)
+        first_col = [(LAST - a) * T for a in range(A)]
+        token_plane_shared = keep.tile([P, WINDOW], U8, name="token_plane_shared", tag="shared_plane", align_bytes=64)
+        token_plane_last = keep.tile([P, WINDOW], U8, name="token_plane_last", align_bytes=64)
+        slot_words = {a: keep.tile([P, S], I32, name=f"slot_words{a}", align_bytes=64) for a in (0, 1, 3, 4)}
+        slot_plane_shared = keep.tile([P, S], U8, name="slot_plane_shared", align_bytes=64)
+        slot_plane_last = keep.tile([P, S], U8, name="slot_plane_last", align_bytes=64)
+        shifted = {a: keep.tile([P, S], U8, name=f"shifted{a}", align_bytes=64) for a in (1, 2, 3)}
         w_planes = keep.tile([P, E * A * N], U8, name="w_planes", align_bytes=64)
-        early = [keep.tile([P, R, 4 * U], F32, name=f"early{h}") for h in range(2)]
-        last = [keep.tile([P, R, 2 * U], F32, name=f"last{h}") for h in range(2)]
-        accs = {(g, h): psum.tile([P, 2 * C], F32, name=f"acc{g}{h}") for g in range(3) for h in range(2)}
+        early = [keep.tile([P, R, 4 * U], F32, name=f"early{h}") for h in range(HALVES)]
+        late = [keep.tile([P, R, 2 * U], F32, name=f"late{h}") for h in range(HALVES)]
+        accs = {(g, h): psum.tile([P, 2 * C], F32, name=f"acc{g}{h}") for g in range(PAIRS) for h in range(HALVES)}
         raw = {}
         weights = {}
 
@@ -54,21 +57,21 @@ def tile_moe_eps_lin_none_kernel(tc, xT, w_words, w_scales, offs, out):
             raw[a] = keep.tile([P, 4, T], F32, name=f"raw{a}", tag=f"raw{a}", align_bytes=64)
             nc.sync.dma_start(out=raw[a][:], in_=xT[512 * a : 512 * (a + 1), :].rearrange("(p j) t -> p j t", j=4))
 
-        def load_pass(a, part):
+        def load_weights_of_pass(a, room, e0, e1):
             nc.sync.dma_start(
-                out=part.bitcast(I32).rearrange("p (e n) -> p e n", e=E),
-                in_=w_words[:, a].bitcast(I32).rearrange("e p n -> p e n"),
+                out=room[:, e0 * W : e1 * W].bitcast(I32).rearrange("p (e n) -> p e n", e=e1 - e0),
+                in_=w_words[e0:e1, a].bitcast(I32).rearrange("e p n -> p e n"),
             )
-            for e in range(E):
-                weights[e, a] = part[:, e * W : (e + 1) * W]
+            for e in range(e0, e1):
+                weights[e, a] = room[:, e * W : (e + 1) * W]
 
-        def load_last_passes(e, part):
+        def load_weights_from_pass_2(e, room):
             nc.sync.dma_start(
-                out=part.bitcast(I32).rearrange("p (a n) -> p a n", a=3),
+                out=room.bitcast(I32).rearrange("p (a n) -> p a n", a=A - 2),
                 in_=w_words[e, 2:A].bitcast(I32).rearrange("a p n -> p a n"),
             )
             for a in range(2, A):
-                weights[e, a] = part[:, (a - 2) * W : (a - 1) * W]
+                weights[e, a] = room[:, (a - 2) * W : (a - 1) * W]
 
         def interleave(a, engine_copy, lo, hi):
             engine_copy(
@@ -77,27 +80,29 @@ def tile_moe_eps_lin_none_kernel(tc, xT, w_words, w_scales, offs, out):
             )
 
         def quantise(a):
-            cut = SCALAR_COLS[a]
+            cut = SCALAR_TOKENS[a]
             interleave(a, nc.scalar.copy, 0, cut)
             if cut < T:
                 interleave(a, nc.vector.tensor_copy, cut, T)
-            for lo, hi in ((0, 512), (512, T)):
-                plane = packed[FIRST_ROW[a] : P, lo:hi] if a in FIRST_ROW else single[a][:, lo:hi]
-                nc.vector.quantize_mx(out=codes[a][:, lo:hi].bitcast(FP8X4), scales=plane, in_=grouped[a][:, 4 * lo : 4 * hi])
+            for lo, hi in QUANTISE_CUTS:
+                nc.vector.quantize_mx(
+                    out=token_words[:, first_col[a] + lo : first_col[a] + hi].bitcast(FP8X4),
+                    scales=token_plane_shared[4 * a : P, lo:hi] if a < LAST else token_plane_last[:, lo:hi],
+                    in_=grouped[a][:, 4 * lo : 4 * hi],
+                )
 
         def gather_words(a, lo, hi):
-            nc.vector.tensor_copy(
-                slot_words[a][:, lo:hi].bitcast(U32),
-                all_codes[:, (A - 1 - a) * T : (A - 1 - a) * T + WINDOW].bitcast(U32).indirect(offsets[:, lo // 16 : hi // 16]),
-            )
+            window = token_words[:, first_col[a] : first_col[a] + WINDOW].bitcast(U32)
+            nc.vector.tensor_copy(slot_words[a][:, lo:hi].bitcast(U32), window.indirect(offsets[:, lo // 16 : hi // 16]))
 
-        def gather_bytes(dst, src, lo, hi):
-            nc.vector.tensor_copy(dst[:, lo:hi], src[:].indirect(offsets[:, lo // 16 : hi // 16]))
+        def gather_bytes(slot_plane, token_plane, lo, hi):
+            nc.vector.tensor_copy(slot_plane[:, lo:hi], token_plane[:].indirect(offsets[:, lo // 16 : hi // 16]))
 
         nc.vector.memset(w_planes[:].bitcast(I32), 0)
-        for plane in [packed, single[3], single[4], shifted[1], shifted[2]]:
+        for plane in [token_plane_shared, token_plane_last, shifted[1], shifted[2], shifted[3]]:
             nc.vector.memset(plane[:].bitcast(I32), 0)
-        nc.vector.memset(all_codes[:, A * T :], 0)
+        nc.vector.memset(token_words[:, A * T :], 0)
+
         load_x(0)
         nc.sync.dma_start(offsets[:], offs)
         for a in range(1, A):
@@ -107,49 +112,53 @@ def tile_moe_eps_lin_none_kernel(tc, xT, w_words, w_scales, offs, out):
                 out=w_planes[r:P:32, :].bitcast(I32).rearrange("q (g n) -> q g n", g=E * A),
                 in_=w_scales[:, :, r:16:4, :].bitcast(I32).rearrange("e a q n -> q (e a) n"),
             )
-        for a in range(A):
-            quantise(a)
-            if a == 0:
-                first_weights = keep.tile([P, E * W], U8, name="first_weights", tag="raw0", align_bytes=64)
-                load_pass(0, first_weights[:])
-            if a == 2:
-                gather_bytes(slot_packed, packed, 0, S)
-                for b in (1, 2):
-                    first = FIRST_ROW[b]
-                    nc.sync.dma_start(
-                        out=shifted[b][0:SHIFT_ROWS, :].bitcast(I32),
-                        in_=slot_packed[first : first + SHIFT_ROWS, :].bitcast(I32),
-                    )
-                held = keep.tile([P, E * (A - 1) * W], U8, name="weights", tag="late", align_bytes=64)
-                load_pass(1, held[:, 0 : E * W])
-                for e in range(E):
-                    load_last_passes(e, held[:, (E + 3 * e) * W : (E + 3 * e + 3) * W])
-            if a < 4:
-                gather_words(a, 0, S)
-            if a == 3:
-                gather_bytes(slot_single[a], single[a], 0, S)
-        for lo in (0, 256, 512):
-            gather_bytes(slot_single[4], single[4], lo, lo + 256)
-            gather_words(4, lo, lo + 256)
 
-        planes = [slot_packed, shifted[1], shifted[2], slot_single[3], slot_single[4]]
+        quantise(0)
+        weights_01 = keep.tile([P, 2 * E * W], U8, name="weights_01", tag="raw0", align_bytes=64)
+        for g in range(PAIRS):
+            load_weights_of_pass(0, weights_01[:, 0 : E * W], 2 * g, 2 * g + 2)
+        load_weights_of_pass(1, weights_01[:, E * W : 2 * E * W], 0, E)
+        gather_words(0, 0, S)
+        quantise(1)
+        gather_words(1, 0, S)
+        quantise(2)
+        quantise(3)
+
+        gather_bytes(slot_plane_shared, token_plane_shared, 0, S)
+        for a in (1, 2, 3):
+            nc.sync.dma_start(
+                out=shifted[a][0:SHIFT_ROWS, :].bitcast(I32),
+                in_=slot_plane_shared[4 * a : 4 * a + SHIFT_ROWS, :].bitcast(I32),
+            )
+        weights_234 = keep.tile([P, E * (A - 2) * W], U8, name="weights_234", tag="shared_plane", align_bytes=64)
+        for e in range(E):
+            load_weights_from_pass_2(e, weights_234[:, (A - 2) * e * W : (A - 2) * (e + 1) * W])
+        slot_words[2] = keep.tile([P, S], I32, name="slot_words2", tag="grouped3", align_bytes=64)
+        gather_words(2, 0, S)
+        gather_words(3, 0, S)
+
+        quantise(LAST)
+        for g in range(PAIRS):
+            gather_bytes(slot_plane_last, token_plane_last, 2 * C * g, 2 * C * (g + 1))
+            gather_words(LAST, 2 * C * g, 2 * C * (g + 1))
+
+        slot_planes = [slot_plane_shared, shifted[1], shifted[2], shifted[3], slot_plane_last]
 
         def multiply(e, h, a):
-            words = weights[e, a][:, 256 * h : 256 * h + 256]
-            col = (e * A + a) * N + 128 * h
+            col = (e * A + a) * N + P * h
             slots = slice(C * e, C * (e + 1))
             nc.tensor.matmul_mx(
                 out=accs[e // 2, h][:, C * (e % 2) : C * (e % 2 + 1)],
-                lhsT=words.bitcast(FP4X4),
-                lhsT_scale=w_planes[:, col : col + 128],
+                lhsT=weights[e, a][:, 2 * P * h : 2 * P * (h + 1)].bitcast(FP4X4),
+                lhsT_scale=w_planes[:, col : col + P],
                 rhs=slot_words[a][:, slots].bitcast(FP8X4),
-                rhs_scale=planes[a][:, slots],
+                rhs_scale=slot_planes[a][:, slots],
                 start=(a == 0 and e % 2 == 0),
-                stop=(a == A - 1 and e % 2 == 1),
+                stop=(a == LAST and e % 2 == 1),
             )
 
         def leave(g, h, engine_copy):
-            dst = early[h][:, :, 2 * U * g : 2 * U * (g + 1)] if g < 2 else last[h][:]
+            dst = early[h][:, :, 2 * U * g : 2 * U * (g + 1)] if g < PAIRS - 1 else late[h][:]
             engine_copy(
                 out=dst.rearrange("p m (e u) -> p m e u", e=2),
                 in_=accs[g, h][:].rearrange("p (e m u) -> p m e u", e=2, m=R),
@@ -158,18 +167,18 @@ def tile_moe_eps_lin_none_kernel(tc, xT, w_words, w_scales, offs, out):
         by_rank = out.rearrange("n (m c) -> n m c", m=R)
         for a in (0, 1):
             for e in range(E):
-                for h in range(2):
+                for h in range(HALVES):
                     multiply(e, h, a)
-        for g in range(3):
+        for g in range(PAIRS):
             for e in (2 * g, 2 * g + 1):
                 for a in (2, 3):
-                    for h in range(2):
+                    for h in range(HALVES):
                         multiply(e, h, a)
-            for h in range(2):
+            for h in range(HALVES):
                 for e in (2 * g, 2 * g + 1):
-                    multiply(e, h, 4)
-                leave(g, h, nc.vector.tensor_copy if (g, h) == (2, 1) else nc.scalar.copy)
-                if g == 1:
+                    multiply(e, h, LAST)
+                leave(g, h, nc.vector.tensor_copy if (g, h) == (PAIRS - 1, HALVES - 1) else nc.scalar.copy)
+                if g == PAIRS - 2:
                     nc.sync.dma_start(out=by_rank[P * h : P * (h + 1), :, 0 : 4 * U], in_=early[h][:])
-        nc.scalar.dma_start(out=by_rank[0:P, :, 4 * U : 6 * U], in_=last[0][:])
-        nc.sync.dma_start(out=by_rank[P : 2 * P, :, 4 * U : 6 * U], in_=last[1][:])
+        nc.scalar.dma_start(out=by_rank[0:P, :, 4 * U : 6 * U], in_=late[0][:])
+        nc.sync.dma_start(out=by_rank[P : 2 * P, :, 4 * U : 6 * U], in_=late[1][:])

@@ -125,13 +125,13 @@ def tile_moe_eps_lin_none_kernel(tc, xT, w_words, w_scales, offs, out):
         quantise(3)
 
         gather_bytes(slot_plane_shared, token_plane_shared, 0, S)
-        for a in (1, 2, 3):
-            nc.sync.dma_start(
-                out=shifted[a][0:SHIFT_ROWS, :].bitcast(I32),
-                in_=slot_plane_shared[4 * a : 4 * a + SHIFT_ROWS, :].bitcast(I32),
-            )
         weights_234 = keep.tile([P, E * (A - 2) * W], U8, name="weights_234", tag="shared_plane", align_bytes=64)
         for e in range(E):
+            if e + 1 < LAST:
+                nc.sync.dma_start(
+                    out=shifted[e + 1][0:SHIFT_ROWS, :].bitcast(I32),
+                    in_=slot_plane_shared[4 * (e + 1) : 4 * (e + 1) + SHIFT_ROWS, :].bitcast(I32),
+                )
             load_weights_from_pass_2(e, weights_234[:, (A - 2) * e * W : (A - 2) * (e + 1) * W])
         slot_words[2] = keep.tile([P, S], I32, name="slot_words2", tag="grouped3", align_bytes=64)
         gather_words(2, 0, S)
@@ -140,7 +140,9 @@ def tile_moe_eps_lin_none_kernel(tc, xT, w_words, w_scales, offs, out):
         quantise(LAST)
         for g in range(PAIRS):
             gather_bytes(slot_plane_last, token_plane_last, 2 * C * g, 2 * C * (g + 1))
-            gather_words(LAST, 2 * C * g, 2 * C * (g + 1))
+            step = 2 * C if g < PAIRS - 1 else C
+            for lo in range(2 * C * g, 2 * C * (g + 1), step):
+                gather_words(LAST, lo, lo + step)
 
         slot_planes = [slot_plane_shared, shifted[1], shifted[2], shifted[3], slot_plane_last]
 
@@ -170,13 +172,14 @@ def tile_moe_eps_lin_none_kernel(tc, xT, w_words, w_scales, offs, out):
                 for h in range(HALVES):
                     multiply(e, h, a)
         for g in range(PAIRS):
-            for e in (2 * g, 2 * g + 1):
-                for a in (2, 3):
-                    for h in range(HALVES):
-                        multiply(e, h, a)
+            even, odd = 2 * g, 2 * g + 1
+            first = [(even, 2), (odd, 2), (even, 3), (odd, 3), (even, LAST)] if g == 0 else [(even, 2), (even, 3), (even, LAST)]
+            for e, a in first:
+                for h in range(HALVES):
+                    multiply(e, h, a)
             for h in range(HALVES):
-                for e in (2 * g, 2 * g + 1):
-                    multiply(e, h, LAST)
+                for a in (LAST,) if g == 0 else (2, 3, LAST):
+                    multiply(odd, h, a)
                 leave(g, h, nc.vector.tensor_copy if (g, h) == (PAIRS - 1, HALVES - 1) else nc.scalar.copy)
                 if g == PAIRS - 2:
                     nc.sync.dma_start(out=by_rank[P * h : P * (h + 1), :, 0 : 4 * U], in_=early[h][:])

@@ -12,6 +12,8 @@ W = 2 * N
 PAIRS = E // 2
 HALVES = N // P
 LAST = A - 1
+SPLIT = 3
+AHEAD = 3
 
 F32 = mybir.dt.float32
 BF16 = mybir.dt.bfloat16
@@ -24,7 +26,7 @@ FP4X4 = mybir.dt.float4_e2m1fn_x4
 
 FLOPS = 2 * K * N * S
 
-SCALAR_TOKENS = [224, 384, 448, 256, 640]
+SCALAR_TOKENS = [224, 384, 448, 512, 544]
 WINDOW = 1024
 SHIFT_ROWS = 112
 QUANTISE_CUTS = ((0, 512), (512, T))
@@ -40,15 +42,12 @@ def tile_moe_eps_lin_none_kernel(tc, xT, w_words, w_scales, offs, out):
         grouped = [keep.tile([P, T * 4], BF16, name=f"grouped{a}", tag=f"grouped{a}", align_bytes=64) for a in range(A)]
         token_words = keep.tile([P, LAST * T + WINDOW], I32, name="token_words", align_bytes=64)
         first_col = [(LAST - a) * T for a in range(A)]
-        token_plane_shared = keep.tile([P, WINDOW], U8, name="token_plane_shared", tag="shared_plane", align_bytes=64)
-        token_plane_last = keep.tile([P, WINDOW], U8, name="token_plane_last", align_bytes=64)
-        slot_words = {a: keep.tile([P, S], I32, name=f"slot_words{a}", align_bytes=64) for a in (0, 1, 3, 4)}
-        slot_plane_shared = keep.tile([P, S], U8, name="slot_plane_shared", align_bytes=64)
-        slot_plane_last = keep.tile([P, S], U8, name="slot_plane_last", align_bytes=64)
-        shifted = {a: keep.tile([P, S], U8, name=f"shifted{a}", align_bytes=64) for a in (1, 2, 3)}
+        token_planes = [keep.tile([P, WINDOW], U8, name=f"token_plane{i}", tag=f"token_plane{i}", align_bytes=64) for i in range(2)]
+        slot_words = {a: keep.tile([P, S], I32, name=f"slot_words{a}", align_bytes=64) for a in (0, 1, 4)}
+        packed = [keep.tile([P, S], U8, name=f"packed{i}", align_bytes=64) for i in range(2)]
+        shifted = {a: keep.tile([P, S], U8, name=f"shifted{a}", align_bytes=64) for a in (1, 2, 4)}
         w_planes = keep.tile([P, E * A * N], U8, name="w_planes", align_bytes=64)
-        early = [keep.tile([P, R, 4 * U], F32, name=f"early{h}") for h in range(HALVES)]
-        late = [keep.tile([P, R, 2 * U], F32, name=f"late{h}") for h in range(HALVES)]
+        results = [keep.tile([P, R, E * U], F32, name=f"results{h}") for h in range(HALVES)]
         accs = {(g, h): psum.tile([P, 2 * C], F32, name=f"acc{g}{h}") for g in range(PAIRS) for h in range(HALVES)}
         raw = {}
         weights = {}
@@ -57,21 +56,20 @@ def tile_moe_eps_lin_none_kernel(tc, xT, w_words, w_scales, offs, out):
             raw[a] = keep.tile([P, 4, T], F32, name=f"raw{a}", tag=f"raw{a}", align_bytes=64)
             nc.sync.dma_start(out=raw[a][:], in_=xT[512 * a : 512 * (a + 1), :].rearrange("(p j) t -> p j t", j=4))
 
-        def load_weights_of_pass(a, room, e0, e1):
+        def load_weights(e, a0, a1, room):
             nc.sync.dma_start(
-                out=room[:, e0 * W : e1 * W].bitcast(I32).rearrange("p (e n) -> p e n", e=e1 - e0),
-                in_=w_words[e0:e1, a].bitcast(I32).rearrange("e p n -> p e n"),
+                out=room.bitcast(I32).rearrange("p (a n) -> p a n", a=a1 - a0),
+                in_=w_words[e, a0:a1].bitcast(I32).rearrange("a p n -> p a n"),
             )
-            for e in range(e0, e1):
-                weights[e, a] = room[:, e * W : (e + 1) * W]
+            for a in range(a0, a1):
+                weights[e, a] = room[:, (a - a0) * W : (a - a0 + 1) * W]
 
-        def load_weights_from_pass_2(e, room):
+        def shift(a):
+            row = 4 * (a % SPLIT)
             nc.sync.dma_start(
-                out=room.bitcast(I32).rearrange("p (a n) -> p a n", a=A - 2),
-                in_=w_words[e, 2:A].bitcast(I32).rearrange("a p n -> p a n"),
+                out=shifted[a][0:SHIFT_ROWS, :].bitcast(I32),
+                in_=packed[a // SPLIT][row : row + SHIFT_ROWS, :].bitcast(I32),
             )
-            for a in range(2, A):
-                weights[e, a] = room[:, (a - 2) * W : (a - 1) * W]
 
         def interleave(a, engine_copy, lo, hi):
             engine_copy(
@@ -87,7 +85,7 @@ def tile_moe_eps_lin_none_kernel(tc, xT, w_words, w_scales, offs, out):
             for lo, hi in QUANTISE_CUTS:
                 nc.vector.quantize_mx(
                     out=token_words[:, first_col[a] + lo : first_col[a] + hi].bitcast(FP8X4),
-                    scales=token_plane_shared[4 * a : P, lo:hi] if a < LAST else token_plane_last[:, lo:hi],
+                    scales=token_planes[a // SPLIT][4 * (a % SPLIT) : P, lo:hi],
                     in_=grouped[a][:, 4 * lo : 4 * hi],
                 )
 
@@ -99,7 +97,7 @@ def tile_moe_eps_lin_none_kernel(tc, xT, w_words, w_scales, offs, out):
             nc.vector.tensor_copy(slot_plane[:, lo:hi], token_plane[:].indirect(offsets[:, lo // 16 : hi // 16]))
 
         nc.vector.memset(w_planes[:].bitcast(I32), 0)
-        for plane in [token_plane_shared, token_plane_last, shifted[1], shifted[2], shifted[3]]:
+        for plane in token_planes + list(shifted.values()):
             nc.vector.memset(plane[:].bitcast(I32), 0)
         nc.vector.memset(token_words[:, A * T :], 0)
 
@@ -114,37 +112,36 @@ def tile_moe_eps_lin_none_kernel(tc, xT, w_words, w_scales, offs, out):
             )
 
         quantise(0)
-        weights_01 = keep.tile([P, 2 * E * W], U8, name="weights_01", tag="raw0", align_bytes=64)
-        for g in range(PAIRS):
-            load_weights_of_pass(0, weights_01[:, 0 : E * W], 2 * g, 2 * g + 2)
-        load_weights_of_pass(1, weights_01[:, E * W : 2 * E * W], 0, E)
+        first, rest = SPLIT * W, (A - SPLIT) * W
+        head_weights = keep.tile([P, first], U8, name="head_weights", tag="raw0", align_bytes=64)
+        load_weights(0, 0, SPLIT, head_weights[:])
         gather_words(0, 0, S)
         quantise(1)
         gather_words(1, 0, S)
         quantise(2)
+        gather_bytes(packed[0], token_planes[0], 0, S)
+        shift(1)
+        shift(2)
+        early_weights = keep.tile([P, E * first + AHEAD * rest], U8, name="early_weights", tag="token_plane0", align_bytes=64)
+        for e in range(1, E):
+            load_weights(e, 0, SPLIT, early_weights[:, e * first : (e + 1) * first])
+        for e in range(AHEAD):
+            load_weights(e, SPLIT, A, early_weights[:, E * first + e * rest : E * first + (e + 1) * rest])
         quantise(3)
-
-        gather_bytes(slot_plane_shared, token_plane_shared, 0, S)
-        weights_234 = keep.tile([P, E * (A - 2) * W], U8, name="weights_234", tag="shared_plane", align_bytes=64)
-        for e in range(E):
-            if e + 1 < LAST:
-                nc.sync.dma_start(
-                    out=shifted[e + 1][0:SHIFT_ROWS, :].bitcast(I32),
-                    in_=slot_plane_shared[4 * (e + 1) : 4 * (e + 1) + SHIFT_ROWS, :].bitcast(I32),
-                )
-            load_weights_from_pass_2(e, weights_234[:, (A - 2) * e * W : (A - 2) * (e + 1) * W])
         slot_words[2] = keep.tile([P, S], I32, name="slot_words2", tag="grouped3", align_bytes=64)
         gather_words(2, 0, S)
+        quantise(4)
+        gather_bytes(packed[1], token_planes[1], 0, S)
+        shift(4)
+        late_weights = keep.tile([P, (E - AHEAD) * rest], U8, name="late_weights", tag="token_plane1", align_bytes=64)
+        for e in range(AHEAD, E):
+            load_weights(e, SPLIT, A, late_weights[:, (e - AHEAD) * rest : (e - AHEAD + 1) * rest])
+        slot_words[3] = keep.tile([P, S], I32, name="slot_words3", tag="grouped4", align_bytes=64)
         gather_words(3, 0, S)
-
-        quantise(LAST)
         for g in range(PAIRS):
-            gather_bytes(slot_plane_last, token_plane_last, 2 * C * g, 2 * C * (g + 1))
-            step = 2 * C if g < PAIRS - 1 else C
-            for lo in range(2 * C * g, 2 * C * (g + 1), step):
-                gather_words(LAST, lo, lo + step)
+            gather_words(4, 2 * C * g, 2 * C * (g + 1))
 
-        slot_planes = [slot_plane_shared, shifted[1], shifted[2], shifted[3], slot_plane_last]
+        slot_planes = [packed[0], shifted[1], shifted[2], packed[1], shifted[4]]
 
         def multiply(e, h, a):
             col = (e * A + a) * N + P * h
@@ -160,28 +157,26 @@ def tile_moe_eps_lin_none_kernel(tc, xT, w_words, w_scales, offs, out):
             )
 
         def leave(g, h, engine_copy):
-            dst = early[h][:, :, 2 * U * g : 2 * U * (g + 1)] if g < PAIRS - 1 else late[h][:]
+            dst = results[h][:, :, 2 * U * g : 2 * U * (g + 1)]
             engine_copy(
                 out=dst.rearrange("p m (e u) -> p m e u", e=2),
                 in_=accs[g, h][:].rearrange("p (e m u) -> p m e u", e=2, m=R),
             )
 
+        def both_halves(steps):
+            for e, a in steps:
+                for h in range(HALVES):
+                    multiply(e, h, a)
+
         by_rank = out.rearrange("n (m c) -> n m c", m=R)
-        for a in (0, 1):
-            for e in range(E):
-                for h in range(HALVES):
-                    multiply(e, h, a)
+        both_halves([(e, a) for e in range(E) for a in range(SPLIT)])
+        both_halves([(e, 3) for e in range(AHEAD)])
         for g in range(PAIRS):
-            even, odd = 2 * g, 2 * g + 1
-            first = [(even, 2), (odd, 2), (even, 3), (odd, 3), (even, LAST)] if g == 0 else [(even, 2), (even, 3), (even, LAST)]
-            for e, a in first:
-                for h in range(HALVES):
-                    multiply(e, h, a)
+            both_halves([(AHEAD + g, 3), (2 * g, LAST)])
             for h in range(HALVES):
-                for a in (LAST,) if g == 0 else (2, 3, LAST):
-                    multiply(odd, h, a)
+                multiply(2 * g + 1, h, LAST)
                 leave(g, h, nc.vector.tensor_copy if (g, h) == (PAIRS - 1, HALVES - 1) else nc.scalar.copy)
-                if g == PAIRS - 2:
-                    nc.sync.dma_start(out=by_rank[P * h : P * (h + 1), :, 0 : 4 * U], in_=early[h][:])
-        nc.scalar.dma_start(out=by_rank[0:P, :, 4 * U : 6 * U], in_=late[0][:])
-        nc.sync.dma_start(out=by_rank[P : 2 * P, :, 4 * U : 6 * U], in_=late[1][:])
+                if g == 0:
+                    nc.sync.dma_start(out=by_rank[P * h : P * (h + 1), :, 0 : 2 * U], in_=results[h][:, :, 0 : 2 * U])
+        nc.scalar.dma_start(out=by_rank[0:P, :, 2 * U :], in_=results[0][:, :, 2 * U :])
+        nc.sync.dma_start(out=by_rank[P : 2 * P, :, 2 * U :], in_=results[1][:, :, 2 * U :])

@@ -26,9 +26,9 @@ FP4X4 = mybir.dt.float4_e2m1fn_x4
 
 FLOPS = 2 * K * N * S
 
-SCALAR_TOKENS = [224, 384, 448, 512, 544]
+SCALAR_TOKENS = [176, 288, 384, 448, 496]
 WINDOW = 1024
-SHIFT_ROWS = 112
+SHIFT_ROWS = 100
 QUANTISE_CUTS = ((0, 512), (512, T))
 
 

@@ -26,7 +26,7 @@ FP4X4 = mybir.dt.float4_e2m1fn_x4
 
 FLOPS = 2 * K * N * S
 
-SCALAR_TOKENS = [176, 288, 384, 448, 496]
+SCALAR_TOKENS = [224, 448, 544, 640, 640]
 WINDOW = 1024
 SHIFT_ROWS = 100
 QUANTISE_CUTS = ((0, 512), (512, T))

@@ -13,7 +13,8 @@ PAIRS = E // 2
 HALVES = N // P
 LAST = A - 1
 SPLIT = 3
-AHEAD = 3
+FIRST = 2
+HEAD = A + SPLIT
 
 F32 = mybir.dt.float32
 BF16 = mybir.dt.bfloat16
@@ -26,10 +27,10 @@ FP4X4 = mybir.dt.float4_e2m1fn_x4
 
 FLOPS = 2 * K * N * S
 
-SCALAR_TOKENS = [224, 448, 544, 640, 640]
+VECTOR_TOKENS = [416, 256, 160, 0, 160]
 WINDOW = 1024
 SHIFT_ROWS = 100
-QUANTISE_CUTS = ((0, 512), (512, T))
+QUANTISE_CUTS = ((512, T), (0, 512))
 
 
 def tile_moe_eps_lin_none_kernel(tc, xT, w_words, w_scales, offs, out):
@@ -43,26 +44,45 @@ def tile_moe_eps_lin_none_kernel(tc, xT, w_words, w_scales, offs, out):
         token_words = keep.tile([P, LAST * T + WINDOW], I32, name="token_words", align_bytes=64)
         first_col = [(LAST - a) * T for a in range(A)]
         token_planes = [keep.tile([P, WINDOW], U8, name=f"token_plane{i}", tag=f"token_plane{i}", align_bytes=64) for i in range(2)]
-        slot_words = {a: keep.tile([P, S], I32, name=f"slot_words{a}", align_bytes=64) for a in (0, 1, 4)}
+        slot_words = {a: keep.tile([P, S], I32, name=f"slot_words{a}", align_bytes=64) for a in (0, 1, 2, 4)}
         packed = [keep.tile([P, S], U8, name=f"packed{i}", align_bytes=64) for i in range(2)]
         shifted = {a: keep.tile([P, S], U8, name=f"shifted{a}", align_bytes=64) for a in (1, 2, 4)}
-        w_planes = keep.tile([P, E * A * N], U8, name="w_planes", align_bytes=64)
+        first_planes = keep.tile([P, HEAD * N], U8, name="first_planes", align_bytes=64)
         results = [keep.tile([P, R, E * U], F32, name=f"results{h}") for h in range(HALVES)]
         accs = {(g, h): psum.tile([P, 2 * C], F32, name=f"acc{g}{h}") for g in range(PAIRS) for h in range(HALVES)}
         raw = {}
         weights = {}
+        w_planes = {}
 
         def load_x(a):
             raw[a] = keep.tile([P, 4, T], F32, name=f"raw{a}", tag=f"raw{a}", align_bytes=64)
             nc.sync.dma_start(out=raw[a][:], in_=xT[512 * a : 512 * (a + 1), :].rearrange("(p j) t -> p j t", j=4))
 
-        def load_weights(e, a0, a1, room):
+        def load_scales(queue, g0, g1, planes):
+            rows = w_scales.bitcast(I32).rearrange("e a q n -> q (e a) n")
+            for r in range(4):
+                queue.dma_start(
+                    out=planes[r:P:32, :].bitcast(I32).rearrange("q (g n) -> q g n", g=g1 - g0),
+                    in_=rows[r:16:4, g0:g1, :],
+                )
+            for g in range(g0, g1):
+                w_planes[divmod(g, A)] = planes[:, (g - g0) * N : (g - g0 + 1) * N]
+
+        def load_expert(e, room):
             nc.sync.dma_start(
-                out=room.bitcast(I32).rearrange("p (a n) -> p a n", a=a1 - a0),
-                in_=w_words[e, a0:a1].bitcast(I32).rearrange("a p n -> p a n"),
+                out=room.bitcast(I32).rearrange("p (a n) -> p a n", a=SPLIT),
+                in_=w_words[e, 0:SPLIT].bitcast(I32).rearrange("a p n -> p a n"),
             )
-            for a in range(a0, a1):
-                weights[e, a] = room[:, (a - a0) * W : (a - a0 + 1) * W]
+            for a in range(SPLIT):
+                weights[e, a] = room[:, a * W : (a + 1) * W]
+
+        def load_pass(a, e0, e1, room):
+            nc.sync.dma_start(
+                out=room.bitcast(I32).rearrange("p (e n) -> p e n", e=e1 - e0),
+                in_=w_words[e0:e1, a].bitcast(I32).rearrange("e p n -> p e n"),
+            )
+            for e in range(e0, e1):
+                weights[e, a] = room[:, (e - e0) * W : (e - e0 + 1) * W]
 
         def shift(a):
             row = 4 * (a % SPLIT)
@@ -77,11 +97,13 @@ def tile_moe_eps_lin_none_kernel(tc, xT, w_words, w_scales, offs, out):
                 in_=raw[a][:, :, lo:hi].rearrange("p j (c i) -> p c j i", i=4),
             )
 
+        def round_pass(a):
+            cut = VECTOR_TOKENS[a]
+            interleave(a, nc.scalar.copy, cut, T)
+            if cut > 0:
+                interleave(a, nc.vector.tensor_copy, 0, cut)
+
         def quantise(a):
-            cut = SCALAR_TOKENS[a]
-            interleave(a, nc.scalar.copy, 0, cut)
-            if cut < T:
-                interleave(a, nc.vector.tensor_copy, cut, T)
             for lo, hi in QUANTISE_CUTS:
                 nc.vector.quantize_mx(
                     out=token_words[:, first_col[a] + lo : first_col[a] + hi].bitcast(FP8X4),
@@ -93,11 +115,10 @@ def tile_moe_eps_lin_none_kernel(tc, xT, w_words, w_scales, offs, out):
             window = token_words[:, first_col[a] : first_col[a] + WINDOW].bitcast(U32)
             nc.vector.tensor_copy(slot_words[a][:, lo:hi].bitcast(U32), window.indirect(offsets[:, lo // 16 : hi // 16]))
 
-        def gather_bytes(slot_plane, token_plane, lo, hi):
-            nc.vector.tensor_copy(slot_plane[:, lo:hi], token_plane[:].indirect(offsets[:, lo // 16 : hi // 16]))
+        def gather_bytes(i):
+            nc.vector.tensor_copy(packed[i][:], token_planes[i][:].indirect(offsets[:]))
 
-        nc.vector.memset(w_planes[:].bitcast(I32), 0)
-        for plane in token_planes + list(shifted.values()):
+        for plane in token_planes:
             nc.vector.memset(plane[:].bitcast(I32), 0)
         nc.vector.memset(token_words[:, A * T :], 0)
 
@@ -105,37 +126,39 @@ def tile_moe_eps_lin_none_kernel(tc, xT, w_words, w_scales, offs, out):
         nc.sync.dma_start(offsets[:], offs)
         for a in range(1, A):
             load_x(a)
-        for r in range(4):
-            nc.sync.dma_start(
-                out=w_planes[r:P:32, :].bitcast(I32).rearrange("q (g n) -> q g n", g=E * A),
-                in_=w_scales[:, :, r:16:4, :].bitcast(I32).rearrange("e a q n -> q (e a) n"),
-            )
+        load_scales(nc.sync, 0, HEAD, first_planes)
 
+        first = SPLIT * W
+        round_pass(0)
         quantise(0)
-        first, rest = SPLIT * W, (A - SPLIT) * W
-        head_weights = keep.tile([P, first], U8, name="head_weights", tag="raw0", align_bytes=64)
-        load_weights(0, 0, SPLIT, head_weights[:])
+        head_weights = keep.tile([P, FIRST * first], U8, name="head_weights", tag="raw0", align_bytes=64)
+        for e in range(FIRST):
+            load_expert(e, head_weights[:, e * first : (e + 1) * first])
         gather_words(0, 0, S)
+        round_pass(1)
         quantise(1)
         gather_words(1, 0, S)
+        round_pass(2)
         quantise(2)
-        gather_bytes(packed[0], token_planes[0], 0, S)
+        other_planes = keep.tile([P, (E * A - HEAD) * N], U8, name="other_planes", tag="grouped2", align_bytes=64)
+        load_scales(nc.gpsimd, HEAD, E * A, other_planes)
+        gather_bytes(0)
         shift(1)
         shift(2)
-        early_weights = keep.tile([P, E * first + AHEAD * rest], U8, name="early_weights", tag="token_plane0", align_bytes=64)
-        for e in range(1, E):
-            load_weights(e, 0, SPLIT, early_weights[:, e * first : (e + 1) * first])
-        for e in range(AHEAD):
-            load_weights(e, SPLIT, A, early_weights[:, E * first + e * rest : E * first + (e + 1) * rest])
-        quantise(3)
-        slot_words[2] = keep.tile([P, S], I32, name="slot_words2", tag="grouped3", align_bytes=64)
+        early_weights = keep.tile([P, (E - FIRST) * first + E * W], U8, name="early_weights", tag="token_plane0", align_bytes=64)
+        for e in range(FIRST, E):
+            load_expert(e, early_weights[:, (e - FIRST) * first : (e - FIRST + 1) * first])
+        load_pass(3, 0, E, early_weights[:, (E - FIRST) * first :])
         gather_words(2, 0, S)
+        round_pass(3)
+        round_pass(4)
+        quantise(3)
         quantise(4)
-        gather_bytes(packed[1], token_planes[1], 0, S)
+        gather_bytes(1)
         shift(4)
-        late_weights = keep.tile([P, (E - AHEAD) * rest], U8, name="late_weights", tag="token_plane1", align_bytes=64)
-        for e in range(AHEAD, E):
-            load_weights(e, SPLIT, A, late_weights[:, (e - AHEAD) * rest : (e - AHEAD + 1) * rest])
+        late_weights = keep.tile([P, E * W], U8, name="late_weights", tag="token_plane1", align_bytes=64)
+        for g in range(PAIRS):
+            load_pass(LAST, 2 * g, 2 * g + 2, late_weights[:, 2 * g * W : (2 * g + 2) * W])
         slot_words[3] = keep.tile([P, S], I32, name="slot_words3", tag="grouped4", align_bytes=64)
         gather_words(3, 0, S)
         for g in range(PAIRS):
@@ -144,12 +167,11 @@ def tile_moe_eps_lin_none_kernel(tc, xT, w_words, w_scales, offs, out):
         slot_planes = [packed[0], shifted[1], shifted[2], packed[1], shifted[4]]
 
         def multiply(e, h, a):
-            col = (e * A + a) * N + P * h
             slots = slice(C * e, C * (e + 1))
             nc.tensor.matmul_mx(
                 out=accs[e // 2, h][:, C * (e % 2) : C * (e % 2 + 1)],
                 lhsT=weights[e, a][:, 2 * P * h : 2 * P * (h + 1)].bitcast(FP4X4),
-                lhsT_scale=w_planes[:, col : col + P],
+                lhsT_scale=w_planes[e, a][:, P * h : P * (h + 1)],
                 rhs=slot_words[a][:, slots].bitcast(FP8X4),
                 rhs_scale=slot_planes[a][:, slots],
                 start=(a == 0 and e % 2 == 0),
@@ -170,9 +192,9 @@ def tile_moe_eps_lin_none_kernel(tc, xT, w_words, w_scales, offs, out):
 
         by_rank = out.rearrange("n (m c) -> n m c", m=R)
         both_halves([(e, a) for e in range(E) for a in range(SPLIT)])
-        both_halves([(e, 3) for e in range(AHEAD)])
+        both_halves([(e, 3) for e in (1, 0, 2, 3, 4, 5)])
         for g in range(PAIRS):
-            both_halves([(AHEAD + g, 3), (2 * g, LAST)])
+            both_halves([(2 * g, LAST)])
             for h in range(HALVES):
                 multiply(2 * g + 1, h, LAST)
                 leave(g, h, nc.vector.tensor_copy if (g, h) == (PAIRS - 1, HALVES - 1) else nc.scalar.copy)

@@ -13,8 +13,7 @@ PAIRS = E // 2
 HALVES = N // P
 LAST = A - 1
 SPLIT = 3
-FIRST = 2
-HEAD = A + SPLIT
+TEAM = E // 2
 
 F32 = mybir.dt.float32
 BF16 = mybir.dt.bfloat16
@@ -29,7 +28,6 @@ FLOPS = 2 * K * N * S
 
 VECTOR_TOKENS = [416, 256, 160, 0, 160]
 WINDOW = 1024
-SHIFT_ROWS = 100
 QUANTISE_CUTS = ((512, T), (0, 512))
 
 
@@ -47,26 +45,15 @@ def tile_moe_eps_lin_none_kernel(tc, xT, w_words, w_scales, offs, out):
         slot_words = {a: keep.tile([P, S], I32, name=f"slot_words{a}", align_bytes=64) for a in (0, 1, 2, 4)}
         packed = [keep.tile([P, S], U8, name=f"packed{i}", align_bytes=64) for i in range(2)]
         shifted = {a: keep.tile([P, S], U8, name=f"shifted{a}", align_bytes=64) for a in (1, 2, 4)}
-        first_planes = keep.tile([P, HEAD * N], U8, name="first_planes", align_bytes=64)
+        w_planes = keep.tile([P, E * A * N], U8, name="w_planes", align_bytes=64)
         results = [keep.tile([P, R, E * U], F32, name=f"results{h}") for h in range(HALVES)]
         accs = {(g, h): psum.tile([P, 2 * C], F32, name=f"acc{g}{h}") for g in range(PAIRS) for h in range(HALVES)}
         raw = {}
         weights = {}
-        w_planes = {}
 
         def load_x(a):
             raw[a] = keep.tile([P, 4, T], F32, name=f"raw{a}", tag=f"raw{a}", align_bytes=64)
             nc.sync.dma_start(out=raw[a][:], in_=xT[512 * a : 512 * (a + 1), :].rearrange("(p j) t -> p j t", j=4))
-
-        def load_scales(queue, g0, g1, planes):
-            rows = w_scales.bitcast(I32).rearrange("e a q n -> q (e a) n")
-            for r in range(4):
-                queue.dma_start(
-                    out=planes[r:P:32, :].bitcast(I32).rearrange("q (g n) -> q g n", g=g1 - g0),
-                    in_=rows[r:16:4, g0:g1, :],
-                )
-            for g in range(g0, g1):
-                w_planes[divmod(g, A)] = planes[:, (g - g0) * N : (g - g0 + 1) * N]
 
         def load_expert(e, room):
             nc.sync.dma_start(
@@ -86,10 +73,11 @@ def tile_moe_eps_lin_none_kernel(tc, xT, w_words, w_scales, offs, out):
 
         def shift(a):
             row = 4 * (a % SPLIT)
-            nc.sync.dma_start(
-                out=shifted[a][0:SHIFT_ROWS, :].bitcast(I32),
-                in_=packed[a // SPLIT][row : row + SHIFT_ROWS, :].bitcast(I32),
-            )
+            for r in range(4):
+                nc.sync.dma_start(
+                    out=shifted[a][r:P:32, :].bitcast(I32),
+                    in_=packed[a // SPLIT][row + r : P : 32, :].bitcast(I32),
+                )
 
         def interleave(a, engine_copy, lo, hi):
             engine_copy(
@@ -126,29 +114,28 @@ def tile_moe_eps_lin_none_kernel(tc, xT, w_words, w_scales, offs, out):
         nc.sync.dma_start(offsets[:], offs)
         for a in range(1, A):
             load_x(a)
-        load_scales(nc.sync, 0, HEAD, first_planes)
-
+        for r in range(4):
+            nc.sync.dma_start(
+                out=w_planes[r:P:32, :].bitcast(I32).rearrange("q (g n) -> q g n", g=E * A),
+                in_=w_scales[:, :, r:16:4, :].bitcast(I32).rearrange("e a q n -> q (e a) n"),
+            )
         first = SPLIT * W
-        round_pass(0)
-        quantise(0)
-        head_weights = keep.tile([P, FIRST * first], U8, name="head_weights", tag="raw0", align_bytes=64)
-        for e in range(FIRST):
-            load_expert(e, head_weights[:, e * first : (e + 1) * first])
-        gather_words(0, 0, S)
-        round_pass(1)
-        quantise(1)
-        gather_words(1, 0, S)
-        round_pass(2)
-        quantise(2)
-        other_planes = keep.tile([P, (E * A - HEAD) * N], U8, name="other_planes", tag="grouped2", align_bytes=64)
-        load_scales(nc.gpsimd, HEAD, E * A, other_planes)
+        head_weights = keep.tile([P, first], U8, name="head_weights", align_bytes=64)
+        load_expert(0, head_weights[:])
+
+        for a in range(SPLIT):
+            round_pass(a)
+            quantise(a)
+            if a < SPLIT - 1:
+                gather_words(a, 0, S)
         gather_bytes(0)
+        early_weights = keep.tile([P, (E - 1) * first + TEAM * W], U8, name="early_weights", tag="token_plane0", align_bytes=64)
         shift(1)
-        shift(2)
-        early_weights = keep.tile([P, (E - FIRST) * first + E * W], U8, name="early_weights", tag="token_plane0", align_bytes=64)
-        for e in range(FIRST, E):
-            load_expert(e, early_weights[:, (e - FIRST) * first : (e - FIRST + 1) * first])
-        load_pass(3, 0, E, early_weights[:, (E - FIRST) * first :])
+        for e in range(1, E):
+            if e == TEAM:
+                shift(2)
+            load_expert(e, early_weights[:, (e - 1) * first : e * first])
+        load_pass(3, 0, TEAM, early_weights[:, (E - 1) * first :])
         gather_words(2, 0, S)
         round_pass(3)
         round_pass(4)
@@ -156,13 +143,14 @@ def tile_moe_eps_lin_none_kernel(tc, xT, w_words, w_scales, offs, out):
         quantise(4)
         gather_bytes(1)
         shift(4)
-        late_weights = keep.tile([P, E * W], U8, name="late_weights", tag="token_plane1", align_bytes=64)
-        for g in range(PAIRS):
-            load_pass(LAST, 2 * g, 2 * g + 2, late_weights[:, 2 * g * W : (2 * g + 2) * W])
+        late_weights = keep.tile([P, (2 * E - TEAM) * W], U8, name="late_weights", tag="token_plane1", align_bytes=64)
+        load_pass(3, TEAM, E, late_weights[:, E * W :])
+        for e0, e1 in ((0, 2), (2, 4), (4, 5), (5, 6)):
+            load_pass(LAST, e0, e1, late_weights[:, e0 * W : e1 * W])
         slot_words[3] = keep.tile([P, S], I32, name="slot_words3", tag="grouped4", align_bytes=64)
         gather_words(3, 0, S)
-        for g in range(PAIRS):
-            gather_words(4, 2 * C * g, 2 * C * (g + 1))
+        gather_words(4, 0, 4 * C)
+        gather_words(4, 4 * C, S)
 
         slot_planes = [packed[0], shifted[1], shifted[2], packed[1], shifted[4]]
 
@@ -171,7 +159,7 @@ def tile_moe_eps_lin_none_kernel(tc, xT, w_words, w_scales, offs, out):
             nc.tensor.matmul_mx(
                 out=accs[e // 2, h][:, C * (e % 2) : C * (e % 2 + 1)],
                 lhsT=weights[e, a][:, 2 * P * h : 2 * P * (h + 1)].bitcast(FP4X4),
-                lhsT_scale=w_planes[e, a][:, P * h : P * (h + 1)],
+                lhsT_scale=w_planes[:, (e * A + a) * N + P * h : (e * A + a) * N + P * (h + 1)],
                 rhs=slot_words[a][:, slots].bitcast(FP8X4),
                 rhs_scale=slot_planes[a][:, slots],
                 start=(a == 0 and e % 2 == 0),
@@ -190,15 +178,14 @@ def tile_moe_eps_lin_none_kernel(tc, xT, w_words, w_scales, offs, out):
                 for h in range(HALVES):
                     multiply(e, h, a)
 
-        by_rank = out.rearrange("n (m c) -> n m c", m=R)
-        both_halves([(e, a) for e in range(E) for a in range(SPLIT)])
-        both_halves([(e, 3) for e in (1, 0, 2, 3, 4, 5)])
+        both_halves([(e, a) for e in range(TEAM) for a in range(2)])
+        both_halves([(e, 2) for e in range(TEAM)])
+        both_halves([(e, a) for e in range(TEAM, E) for a in range(SPLIT)])
+        both_halves([(e, 3) for e in range(E)])
         for g in range(PAIRS):
             both_halves([(2 * g, LAST)])
             for h in range(HALVES):
                 multiply(2 * g + 1, h, LAST)
-                leave(g, h, nc.vector.tensor_copy if (g, h) == (PAIRS - 1, HALVES - 1) else nc.scalar.copy)
-                if g == 0:
-                    nc.sync.dma_start(out=by_rank[P * h : P * (h + 1), :, 0 : 2 * U], in_=results[h][:, :, 0 : 2 * U])
-        nc.scalar.dma_start(out=by_rank[0:P, :, 2 * U :], in_=results[0][:, :, 2 * U :])
-        nc.sync.dma_start(out=by_rank[P : 2 * P, :, 2 * U :], in_=results[1][:, :, 2 * U :])
+                leave(g, h, (nc.scalar.copy, nc.vector.tensor_copy)[h])
+        nc.scalar.dma_start(out=out[0:P, :], in_=results[0][:].rearrange("p m c -> p (m c)"))
+        nc.sync.dma_start(out=out[P : 2 * P, :], in_=results[1][:].rearrange("p m c -> p (m c)"))

@@ -38,21 +38,21 @@ def tile_moe_eps_lin_none_kernel(tc, xT, w_words, w_scales, offs, out):
         psum = ctx.enter_context(tc.psum_pool(name="psum", bufs=1))
 
         offsets = keep.tile([P, S // 16], U16, name="offsets")
-        grouped = [keep.tile([P, T * 4], BF16, name=f"grouped{a}", tag=f"grouped{a}", align_bytes=64) for a in range(A)]
-        token_words = keep.tile([P, LAST * T + WINDOW], I32, name="token_words", align_bytes=64)
+        grouped = [keep.tile([P, T * 4], BF16, name=f"grouped{a}", tag=f"grouped{a}", align_bytes=256) for a in range(A)]
+        token_words = keep.tile([P, LAST * T + WINDOW], I32, name="token_words", align_bytes=256)
         first_col = [(LAST - a) * T for a in range(A)]
-        token_planes = [keep.tile([P, WINDOW], U8, name=f"token_plane{i}", tag=f"token_plane{i}", align_bytes=64) for i in range(2)]
-        slot_words = {a: keep.tile([P, S], I32, name=f"slot_words{a}", align_bytes=64) for a in (0, 1, 2, 4)}
-        packed = [keep.tile([P, S], U8, name=f"packed{i}", align_bytes=64) for i in range(2)]
-        shifted = {a: keep.tile([P, S], U8, name=f"shifted{a}", align_bytes=64) for a in (1, 2, 4)}
-        w_planes = keep.tile([P, E * A * N], U8, name="w_planes", align_bytes=64)
-        results = [keep.tile([P, R, E * U], F32, name=f"results{h}") for h in range(HALVES)]
+        token_planes = [keep.tile([P, WINDOW], U8, name=f"token_plane{i}", tag=f"token_plane{i}", align_bytes=256) for i in range(2)]
+        slot_words = {a: keep.tile([P, S], I32, name=f"slot_words{a}", align_bytes=256) for a in (0, 1, 2, 4)}
+        packed = [keep.tile([P, S], U8, name=f"packed{i}", align_bytes=256) for i in range(2)]
+        shifted = {a: keep.tile([P, S], U8, name=f"shifted{a}", align_bytes=256) for a in (1, 2, 4)}
+        w_planes = keep.tile([P, E * A * N], U8, name="w_planes", align_bytes=256)
+        results = [keep.tile([P, R, E * U], F32, name=f"results{h}", align_bytes=256) for h in range(HALVES)]
         accs = {(g, h): psum.tile([P, 2 * C], F32, name=f"acc{g}{h}") for g in range(PAIRS) for h in range(HALVES)}
         raw = {}
         weights = {}
 
         def load_x(a):
-            raw[a] = keep.tile([P, 4, T], F32, name=f"raw{a}", tag=f"raw{a}", align_bytes=64)
+            raw[a] = keep.tile([P, 4, T], F32, name=f"raw{a}", tag=f"raw{a}", align_bytes=256)
             nc.sync.dma_start(out=raw[a][:], in_=xT[512 * a : 512 * (a + 1), :].rearrange("(p j) t -> p j t", j=4))
 
         def load_expert(e, room):
@@ -120,7 +120,7 @@ def tile_moe_eps_lin_none_kernel(tc, xT, w_words, w_scales, offs, out):
                 in_=w_scales[:, :, r:16:4, :].bitcast(I32).rearrange("e a q n -> q (e a) n"),
             )
         first = SPLIT * W
-        head_weights = keep.tile([P, first], U8, name="head_weights", align_bytes=64)
+        head_weights = keep.tile([P, first], U8, name="head_weights", align_bytes=256)
         load_expert(0, head_weights[:])
 
         for a in range(SPLIT):
@@ -129,7 +129,7 @@ def tile_moe_eps_lin_none_kernel(tc, xT, w_words, w_scales, offs, out):
             if a < SPLIT - 1:
                 gather_words(a, 0, S)
         gather_bytes(0)
-        early_weights = keep.tile([P, (E - 1) * first + TEAM * W], U8, name="early_weights", tag="token_plane0", align_bytes=64)
+        early_weights = keep.tile([P, (E - 1) * first + TEAM * W], U8, name="early_weights", tag="token_plane0", align_bytes=256)
         shift(1)
         for e in range(1, E):
             if e == TEAM:
@@ -143,11 +143,11 @@ def tile_moe_eps_lin_none_kernel(tc, xT, w_words, w_scales, offs, out):
         quantise(4)
         gather_bytes(1)
         shift(4)
-        late_weights = keep.tile([P, (2 * E - TEAM) * W], U8, name="late_weights", tag="token_plane1", align_bytes=64)
+        late_weights = keep.tile([P, (2 * E - TEAM) * W], U8, name="late_weights", tag="token_plane1", align_bytes=256)
         load_pass(3, TEAM, E, late_weights[:, E * W :])
         for e0, e1 in ((0, 2), (2, 4), (4, 5), (5, 6)):
             load_pass(LAST, e0, e1, late_weights[:, e0 * W : e1 * W])
-        slot_words[3] = keep.tile([P, S], I32, name="slot_words3", tag="grouped4", align_bytes=64)
+        slot_words[3] = keep.tile([P, S], I32, name="slot_words3", tag="grouped4", align_bytes=256)
         gather_words(3, 0, S)
         gather_words(4, 0, 4 * C)
         gather_words(4, 4 * C, S)

@@ -26,7 +26,9 @@ FP4X4 = mybir.dt.float4_e2m1fn_x4
 
 FLOPS = 2 * K * N * S
 
-VECTOR_TOKENS = [416, 256, 160, 0, 160]
+VECTOR_TOKENS = [416, 176, 112, 0, 96]
+EARLY = 128
+CUT_PASSES = (1, 2, 3, 4)
 WINDOW = 1024
 QUANTISE_CUTS = ((512, T), (0, 512))
 
@@ -52,8 +54,11 @@ def tile_moe_eps_lin_none_kernel(tc, xT, w_words, w_scales, offs, out):
         weights = {}
 
         def load_x(a):
-            raw[a] = keep.tile([P, 4, T], F32, name=f"raw{a}", tag=f"raw{a}", align_bytes=256)
-            nc.sync.dma_start(out=raw[a][:], in_=xT[512 * a : 512 * (a + 1), :].rearrange("(p j) t -> p j t", j=4))
+            raw[a] = keep.tile([P, 4 * T], F32, name=f"raw{a}", tag=f"raw{a}", align_bytes=256)
+            rows = xT[512 * a : 512 * (a + 1), :].rearrange("(p j) t -> p (j t)", j=4)
+            ends = (0, 3 * T + EARLY, 4 * T) if a in CUT_PASSES else (0, 4 * T)
+            for lo, hi in zip(ends, ends[1:]):
+                nc.sync.dma_start(out=raw[a][:, lo:hi], in_=rows[:, lo:hi])
 
         def load_expert(e, room):
             nc.sync.dma_start(
@@ -82,17 +87,20 @@ def tile_moe_eps_lin_none_kernel(tc, xT, w_words, w_scales, offs, out):
         def interleave(a, engine_copy, lo, hi):
             engine_copy(
                 out=grouped[a][:, 4 * lo : 4 * hi].rearrange("p (c i j) -> p c j i", i=4, j=4),
-                in_=raw[a][:, :, lo:hi].rearrange("p j (c i) -> p c j i", i=4),
+                in_=raw[a][:].rearrange("p (j t) -> p j t", j=4)[:, :, lo:hi].rearrange("p j (c i) -> p c j i", i=4),
             )
 
         def round_pass(a):
-            cut = VECTOR_TOKENS[a]
+            start = EARLY if a in CUT_PASSES else 0
+            cut = start + VECTOR_TOKENS[a]
+            if start > 0:
+                interleave(a, nc.scalar.copy, 0, start)
             interleave(a, nc.scalar.copy, cut, T)
-            if cut > 0:
-                interleave(a, nc.vector.tensor_copy, 0, cut)
+            if cut > start:
+                interleave(a, nc.vector.tensor_copy, start, cut)
 
         def quantise(a):
-            for lo, hi in QUANTISE_CUTS:
+            for lo, hi in ((0, EARLY), (EARLY, T)) if a in CUT_PASSES else QUANTISE_CUTS:
                 nc.vector.quantize_mx(
                     out=token_words[:, first_col[a] + lo : first_col[a] + hi].bitcast(FP8X4),
                     scales=token_planes[a // SPLIT][4 * (a % SPLIT) : P, lo:hi],

@@ -13,7 +13,8 @@ PAIRS = E // 2
 HALVES = N // P
 LAST = A - 1
 SPLIT = 3
-TEAM = E // 2
+TEAM = 4
+AHEAD = E // 2
 
 F32 = mybir.dt.float32
 BF16 = mybir.dt.bfloat16
@@ -128,8 +129,6 @@ def tile_moe_eps_lin_none_kernel(tc, xT, w_words, w_scales, offs, out):
                 in_=w_scales[:, :, r:16:4, :].bitcast(I32).rearrange("e a q n -> q (e a) n"),
             )
         first = SPLIT * W
-        head_weights = keep.tile([P, first], U8, name="head_weights", align_bytes=256)
-        load_expert(0, head_weights[:])
 
         for a in range(SPLIT):
             round_pass(a)
@@ -137,13 +136,13 @@ def tile_moe_eps_lin_none_kernel(tc, xT, w_words, w_scales, offs, out):
             if a < SPLIT - 1:
                 gather_words(a, 0, S)
         gather_bytes(0)
-        early_weights = keep.tile([P, (E - 1) * first + TEAM * W], U8, name="early_weights", tag="token_plane0", align_bytes=256)
+        early_weights = keep.tile([P, E * first + AHEAD * W], U8, name="early_weights", tag="token_plane0", align_bytes=256)
         shift(1)
-        for e in range(1, E):
+        for e in range(E):
             if e == TEAM:
                 shift(2)
-            load_expert(e, early_weights[:, (e - 1) * first : e * first])
-        load_pass(3, 0, TEAM, early_weights[:, (E - 1) * first :])
+            load_expert(e, early_weights[:, e * first : (e + 1) * first])
+        load_pass(3, 0, AHEAD, early_weights[:, E * first :])
         gather_words(2, 0, S)
         round_pass(3)
         round_pass(4)
@@ -151,8 +150,8 @@ def tile_moe_eps_lin_none_kernel(tc, xT, w_words, w_scales, offs, out):
         quantise(4)
         gather_bytes(1)
         shift(4)
-        late_weights = keep.tile([P, (2 * E - TEAM) * W], U8, name="late_weights", tag="token_plane1", align_bytes=256)
-        load_pass(3, TEAM, E, late_weights[:, E * W :])
+        late_weights = keep.tile([P, (2 * E - AHEAD) * W], U8, name="late_weights", tag="token_plane1", align_bytes=256)
+        load_pass(3, AHEAD, E, late_weights[:, E * W :])
         for e0, e1 in ((0, 2), (2, 4), (4, 5), (5, 6)):
             load_pass(LAST, e0, e1, late_weights[:, e0 * W : e1 * W])
         slot_words[3] = keep.tile([P, S], I32, name="slot_words3", tag="grouped4", align_bytes=256)

@@ -27,7 +27,7 @@ FP4X4 = mybir.dt.float4_e2m1fn_x4
 
 FLOPS = 2 * K * N * S
 
-VECTOR_TOKENS = [416, 176, 112, 0, 96]
+VECTOR_TOKENS = [416, 160, 96, 0, 80]
 EARLY = 128
 CUT_PASSES = (1, 2, 3, 4)
 WINDOW = 1024
@@ -61,12 +61,12 @@ def tile_moe_eps_lin_none_kernel(tc, xT, w_words, w_scales, offs, out):
             for lo, hi in zip(ends, ends[1:]):
                 nc.sync.dma_start(out=raw[a][:, lo:hi], in_=rows[:, lo:hi])
 
-        def load_expert(e, room):
+        def load_expert(e, a0, room):
             nc.sync.dma_start(
-                out=room.bitcast(I32).rearrange("p (a n) -> p a n", a=SPLIT),
-                in_=w_words[e, 0:SPLIT].bitcast(I32).rearrange("a p n -> p a n"),
+                out=room[:, a0 * W :].bitcast(I32).rearrange("p (a n) -> p a n", a=SPLIT - a0),
+                in_=w_words[e, a0:SPLIT].bitcast(I32).rearrange("a p n -> p a n"),
             )
-            for a in range(SPLIT):
+            for a in range(a0, SPLIT):
                 weights[e, a] = room[:, a * W : (a + 1) * W]
 
         def load_pass(a, e0, e1, room):
@@ -123,6 +123,8 @@ def tile_moe_eps_lin_none_kernel(tc, xT, w_words, w_scales, offs, out):
         nc.sync.dma_start(offsets[:], offs)
         for a in range(1, A):
             load_x(a)
+        head_weights = keep.tile([P, W], U8, name="head_weights", align_bytes=256)
+        load_pass(0, 0, 1, head_weights[:])
         for r in range(4):
             nc.sync.dma_start(
                 out=w_planes[r:P:32, :].bitcast(I32).rearrange("q (g n) -> q g n", g=E * A),
@@ -141,7 +143,7 @@ def tile_moe_eps_lin_none_kernel(tc, xT, w_words, w_scales, offs, out):
         for e in range(E):
             if e == TEAM:
                 shift(2)
-            load_expert(e, early_weights[:, e * first : (e + 1) * first])
+            load_expert(e, 1 if e == 0 else 0, early_weights[:, e * first : (e + 1) * first])
         load_pass(3, 0, AHEAD, early_weights[:, E * first :])
         gather_words(2, 0, S)
         round_pass(3)
@@ -152,7 +154,7 @@ def tile_moe_eps_lin_none_kernel(tc, xT, w_words, w_scales, offs, out):
         shift(4)
         late_weights = keep.tile([P, (2 * E - AHEAD) * W], U8, name="late_weights", tag="token_plane1", align_bytes=256)
         load_pass(3, AHEAD, E, late_weights[:, E * W :])
-        for e0, e1 in ((0, 2), (2, 4), (4, 5), (5, 6)):
+        for e0, e1 in ((0, 2), (2, 4), (4, 6)):
             load_pass(LAST, e0, e1, late_weights[:, e0 * W : e1 * W])
         slot_words[3] = keep.tile([P, S], I32, name="slot_words3", tag="grouped4", align_bytes=256)
         gather_words(3, 0, S)
@@ -193,6 +195,6 @@ def tile_moe_eps_lin_none_kernel(tc, xT, w_words, w_scales, offs, out):
             both_halves([(2 * g, LAST)])
             for h in range(HALVES):
                 multiply(2 * g + 1, h, LAST)
-                leave(g, h, (nc.scalar.copy, nc.vector.tensor_copy)[h])
+                leave(g, h, nc.vector.tensor_copy if h == 1 and g > 0 else nc.scalar.copy)
         nc.scalar.dma_start(out=out[0:P, :], in_=results[0][:].rearrange("p m c -> p (m c)"))
         nc.sync.dma_start(out=out[P : 2 * P, :], in_=results[1][:].rearrange("p m c -> p (m c)"))

from contextlib import ExitStack

import concourse.mybir as mybir

K, T, E, C, N = 2560, 640, 6, 128, 256
R = 4
S = E * C
P = 128
A = K // 512
U = C // R
W = 2 * N
PAIRS = E // 2
HALVES = N // P
LAST = A - 1
SPLIT = 3
TEAM = 4
AHEAD = E // 2

F32 = mybir.dt.float32
BF16 = mybir.dt.bfloat16
I32 = mybir.dt.int32
U32 = mybir.dt.uint32
U16 = mybir.dt.uint16
U8 = mybir.dt.uint8
FP8X4 = mybir.dt.float8_e4m3fn_x4
FP4X4 = mybir.dt.float4_e2m1fn_x4

FLOPS = 2 * K * N * S

VECTOR_TOKENS = [416, 160, 96, 0, 80]
EARLY = 128
CUT_PASSES = (1, 2, 3, 4)
WINDOW = 1024
QUANTISE_CUTS = ((512, T), (0, 512))


def tile_moe_eps_lin_none_kernel(tc, xT, w_words, w_scales, offs, out):
    nc = tc.nc
    with ExitStack() as ctx:
        keep = ctx.enter_context(tc.tile_pool(name="keep", bufs=1))
        psum = ctx.enter_context(tc.psum_pool(name="psum", bufs=1))

        offsets = keep.tile([P, S // 16], U16, name="offsets")
        grouped = [keep.tile([P, T * 4], BF16, name=f"grouped{a}", tag=f"grouped{a}", align_bytes=256) for a in range(A)]
        token_words = keep.tile([P, LAST * T + WINDOW], I32, name="token_words", align_bytes=256)
        first_col = [(LAST - a) * T for a in range(A)]
        token_planes = [keep.tile([P, WINDOW], U8, name=f"token_plane{i}", tag=f"token_plane{i}", align_bytes=256) for i in range(2)]
        slot_words = {a: keep.tile([P, S], I32, name=f"slot_words{a}", align_bytes=256) for a in (0, 1, 2, 4)}
        packed = [keep.tile([P, S], U8, name=f"packed{i}", align_bytes=256) for i in range(2)]
        shifted = {a: keep.tile([P, S], U8, name=f"shifted{a}", align_bytes=256) for a in (1, 2, 4)}
        w_planes = keep.tile([P, E * A * N], U8, name="w_planes", align_bytes=256)
        results = [keep.tile([P, R, E * U], F32, name=f"results{h}", align_bytes=256) for h in range(HALVES)]
        accs = {(g, h): psum.tile([P, 2 * C], F32, name=f"acc{g}{h}") for g in range(PAIRS) for h in range(HALVES)}
        raw = {}
        weights = {}

        def load_x(a):
            raw[a] = keep.tile([P, 4 * T], F32, name=f"raw{a}", tag=f"raw{a}", align_bytes=256)
            rows = xT[512 * a : 512 * (a + 1), :].rearrange("(p j) t -> p (j t)", j=4)
            ends = (0, 3 * T + EARLY, 4 * T) if a in CUT_PASSES else (0, 4 * T)
            for lo, hi in zip(ends, ends[1:]):
                nc.sync.dma_start(out=raw[a][:, lo:hi], in_=rows[:, lo:hi])

        def load_expert(e, a0, room):
            nc.sync.dma_start(
                out=room[:, a0 * W :].bitcast(I32).rearrange("p (a n) -> p a n", a=SPLIT - a0),
                in_=w_words[e, a0:SPLIT].bitcast(I32).rearrange("a p n -> p a n"),
            )
            for a in range(a0, SPLIT):
                weights[e, a] = room[:, a * W : (a + 1) * W]

        def load_pass(a, e0, e1, room):
            nc.sync.dma_start(
                out=room.bitcast(I32).rearrange("p (e n) -> p e n", e=e1 - e0),
                in_=w_words[e0:e1, a].bitcast(I32).rearrange("e p n -> p e n"),
            )
            for e in range(e0, e1):
                weights[e, a] = room[:, (e - e0) * W : (e - e0 + 1) * W]

        def shift(a):
            row = 4 * (a % SPLIT)
            for r in range(4):
                nc.sync.dma_start(
                    out=shifted[a][r:P:32, :].bitcast(I32),
                    in_=packed[a // SPLIT][row + r : P : 32, :].bitcast(I32),
                )

        def interleave(a, engine_copy, lo, hi):
            engine_copy(
                out=grouped[a][:, 4 * lo : 4 * hi].rearrange("p (c i j) -> p c j i", i=4, j=4),
                in_=raw[a][:].rearrange("p (j t) -> p j t", j=4)[:, :, lo:hi].rearrange("p j (c i) -> p c j i", i=4),
            )

        def round_pass(a):
            start = EARLY if a in CUT_PASSES else 0
            cut = start + VECTOR_TOKENS[a]
            if start > 0:
                interleave(a, nc.scalar.copy, 0, start)
            interleave(a, nc.scalar.copy, cut, T)
            if cut > start:
                interleave(a, nc.vector.tensor_copy, start, cut)

        def quantise(a):
            for lo, hi in ((0, EARLY), (EARLY, T)) if a in CUT_PASSES else QUANTISE_CUTS:
                nc.vector.quantize_mx(
                    out=token_words[:, first_col[a] + lo : first_col[a] + hi].bitcast(FP8X4),
                    scales=token_planes[a // SPLIT][4 * (a % SPLIT) : P, lo:hi],
                    in_=grouped[a][:, 4 * lo : 4 * hi],
                )

        def gather_words(a, lo, hi):
            window = token_words[:, first_col[a] : first_col[a] + WINDOW].bitcast(U32)
            nc.vector.tensor_copy(slot_words[a][:, lo:hi].bitcast(U32), window.indirect(offsets[:, lo // 16 : hi // 16]))

        def gather_bytes(i):
            nc.vector.tensor_copy(packed[i][:], token_planes[i][:].indirect(offsets[:]))

        for plane in token_planes:
            nc.vector.memset(plane[:].bitcast(I32), 0)
        nc.vector.memset(token_words[:, A * T :], 0)

        load_x(0)
        nc.sync.dma_start(offsets[:], offs)
        for a in range(1, A):
            load_x(a)
        head_weights = keep.tile([P, W], U8, name="head_weights", align_bytes=256)
        load_pass(0, 0, 1, head_weights[:])
        for r in range(4):
            nc.sync.dma_start(
                out=w_planes[r:P:32, :].bitcast(I32).rearrange("q (g n) -> q g n", g=E * A),
                in_=w_scales[:, :, r:16:4, :].bitcast(I32).rearrange("e a q n -> q (e a) n"),
            )
        first = SPLIT * W

        for a in range(SPLIT):
            round_pass(a)
            quantise(a)
            if a < SPLIT - 1:
                gather_words(a, 0, S)
        gather_bytes(0)
        early_weights = keep.tile([P, E * first + AHEAD * W], U8, name="early_weights", tag="token_plane0", align_bytes=256)
        shift(1)
        for e in range(E):
            if e == TEAM:
                shift(2)
            load_expert(e, 1 if e == 0 else 0, early_weights[:, e * first : (e + 1) * first])
        load_pass(3, 0, AHEAD, early_weights[:, E * first :])
        gather_words(2, 0, S)
        round_pass(3)
        round_pass(4)
        quantise(3)
        quantise(4)
        gather_bytes(1)
        shift(4)
        late_weights = keep.tile([P, (2 * E - AHEAD) * W], U8, name="late_weights", tag="token_plane1", align_bytes=256)
        load_pass(3, AHEAD, E, late_weights[:, E * W :])
        for e0, e1 in ((0, 2), (2, 4), (4, 6)):
            load_pass(LAST, e0, e1, late_weights[:, e0 * W : e1 * W])
        slot_words[3] = keep.tile([P, S], I32, name="slot_words3", tag="grouped4", align_bytes=256)
        gather_words(3, 0, S)
        gather_words(4, 0, 4 * C)
        gather_words(4, 4 * C, S)

        slot_planes = [packed[0], shifted[1], shifted[2], packed[1], shifted[4]]

        def multiply(e, h, a):
            slots = slice(C * e, C * (e + 1))
            nc.tensor.matmul_mx(
                out=accs[e // 2, h][:, C * (e % 2) : C * (e % 2 + 1)],
                lhsT=weights[e, a][:, 2 * P * h : 2 * P * (h + 1)].bitcast(FP4X4),
                lhsT_scale=w_planes[:, (e * A + a) * N + P * h : (e * A + a) * N + P * (h + 1)],
                rhs=slot_words[a][:, slots].bitcast(FP8X4),
                rhs_scale=slot_planes[a][:, slots],
                start=(a == 0 and e % 2 == 0),
                stop=(a == LAST and e % 2 == 1),
            )

        def leave(g, h, engine_copy):
            dst = results[h][:, :, 2 * U * g : 2 * U * (g + 1)]
            engine_copy(
                out=dst.rearrange("p m (e u) -> p m e u", e=2),
                in_=accs[g, h][:].rearrange("p (e m u) -> p m e u", e=2, m=R),
            )

        def both_halves(steps):
            for e, a in steps:
                for h in range(HALVES):
                    multiply(e, h, a)

        both_halves([(e, a) for e in range(TEAM) for a in range(2)])
        both_halves([(e, 2) for e in range(TEAM)])
        both_halves([(e, a) for e in range(TEAM, E) for a in range(SPLIT)])
        both_halves([(e, 3) for e in range(E)])
        for g in range(PAIRS):
            both_halves([(2 * g, LAST)])
            for h in range(HALVES):
                multiply(2 * g + 1, h, LAST)
                leave(g, h, nc.vector.tensor_copy if h == 1 and g > 0 else nc.scalar.copy)
        nc.scalar.dma_start(out=out[0:P, :], in_=results[0][:].rearrange("p m c -> p (m c)"))
        nc.sync.dma_start(out=out[P : 2 * P, :], in_=results[1][:].rearrange("p m c -> p (m c)"))
